import numpy as np, ml_dtypes
CORES = [13,21,141,149]
N = 4
BF = ml_dtypes.bfloat16
W, A, S, CAP, RO = 2048, 512, 2, 128, 4
P, BL = A // S, W // CAP
WT = 2 * np.arange(16) + 1
def counts(rng, fat):
    return np.where(fat, rng.integers(9, 17, fat.shape), rng.integers(0, 9, fat.shape))
def cols(rng, n, top):
    on = np.argsort(rng.random((N, 8, 16, W)), axis=2) < n[:, :, None, :]
    return np.where(on, 1 + (top * rng.random((N, 8, 16, W))).astype(np.int64), 0)
def lines(rng, fat, share):
    o = np.argsort(np.where(fat, 0.0, 1.0) + 0.5 * rng.random((N, 8, W)), axis=-1); nf = np.add.reduce(fat.astype(np.int64), axis=-1)[:, :, None, None]
    v = rng.random((N, 8, 16, A))
    k = np.where(rng.random((N, 8, 16, A)) < share, (v * nf).astype(np.int64), nf + (v * (W - nf)).astype(np.int64))
    return np.take_along_axis(o, k.reshape(N, 8, 16 * A), 2).reshape(N, 8, 16, A)
def hop(e, u):
    return (((e * u) >> 5) + e) & (W - 1)
def first(X):
    u = np.add.reduce(X * WT.reshape(1, 1, 16, 1), axis=2) & (W - 1); h = hop(np.arange(W).reshape(1, 1, W), u)
    y = np.take_along_axis(X, h[:, :, None, :], 3)
    return np.add.reduce(np.sign(y - X), axis=2), np.add.reduce((X > 0).astype(np.int64), axis=2)
def top16(s):
    v = np.full(16, 255); d = (65280 - s) & (W - 1)
    for w in range(15, -1, -1):
        c = min(254, d // (2 * w + 1)); v[w] -= c; d -= c * (2 * w + 1)
    return v
def pack(X, E, M):
    return {"xt": X.reshape(N, 128, W).astype(np.float32).astype(BF), "led": E.reshape(N, 128, A).astype(np.int32), "mk": M.reshape(N, 128, A).astype(np.float32).astype(BF)}
def setup_inputs(rng):
    fat = rng.random((N, 8, W)) < rng.choice(np.array([0.3, 0.5, 0.7]), (N, 8, 1))
    X = cols(rng, counts(rng, fat), 255)
    share = rng.choice(np.array([0.01, 0.05, 0.15, 0.6]), (N, 8, 1, A)) * rng.choice(np.array([0.2, 1.0, 1.5]), (N, 8, 1, 1))
    return pack(X, lines(rng, fat, share), rng.integers(0, 2, (N, 8, 16, A)))
def setup_inputs_spread(rng):
    fat = rng.random((N, 8, W)) < rng.choice(np.array([0.2, 0.5, 0.8]), (N, 8, 1))
    top = np.minimum(np.exp2(8 * rng.random((N, 8, 1, W))).astype(np.int64), 255)
    X = cols(rng, counts(rng, fat), top)
    E = lines(rng, fat, rng.choice(np.array([0.01, 0.05, 0.2, 0.7]), (N, 8, 1, A)))
    low = (W * rng.random((N, 8, 16, A)) ** 4).astype(np.int64); E = np.where(rng.random((N, 8, 1, A)) < 0.25, low, E)
    return pack(X, E, (rng.random((N, 8, 16, A)) < rng.random((N, 8, 1, A))).astype(np.int64))
def setup_inputs_ends(rng):
    kind = rng.integers(0, 3, (N, 8, 1, W))
    X = np.where(kind == 0, 0, np.where(kind == 1, 255, 255 * rng.integers(0, 2, (N, 8, 16, W))))
    X[..., 1] = 1; X[..., hop(1, 256)] = 255
    X[..., 2] = 255; X[..., hop(2, 65280 & (W - 1))] = 0
    X[..., W - 2] = 254; X[..., hop(W - 2, 65024 & (W - 1))] = 255
    X[..., W - 1] = top16(W - 1); X[..., hop(W - 1, W - 1)] = 0
    sh = (N, 8, 16, A)
    other = np.where(rng.random(sh) < 0.5, rng.choice(np.array([1, 2, W - 2]), sh), rng.integers(0, W, sh))
    E = np.where(rng.random(sh) < 0.7, (W - 1) * rng.integers(0, 2, sh), other)
    M = (rng.random(sh) < rng.choice(np.array([0.0, 0.5, 1.0]), (N, 8, 1, A))).astype(np.int64)
    i = np.arange(P) * S; q = N - 1
    for r in (0, q):
        for g in range(8):
            k = 2 * rng.integers(0, 8, P); E[r, g, k, i] = W - 1; M[r, g, k, i] = 1
    E[1, 0, :, 0::S] = 0; M[1, 0, :, 0::S] = 0
    E[q, 0, :, 0] = 0; M[q, 0, :, 0] = 0
    a, b, c, d = int(i[CAP - 1]), int(i[P - 1]), int(i[P - 2]), int(i[3])
    E[q, 7, :, a] = W - 1; M[q, 7, :, a] = 1
    E[q, 7, :, b] = 0; M[q, 7, :, b] = 0; E[q, 7, 14:, b] = W - 1; M[q, 7, 14:, b] = 1
    E[q, 7, :, c] = 0; M[q, 7, :, c] = 0; E[q, 7, 14, c] = W - 2; M[q, 7, 14, c] = 1; E[q, 7, 15, c] = 1
    E[:, 7, 0::2, d] = 2; M[:, 7, 0::2, d] = 1; E[:, 7, 1::2, d] = W - 1; M[:, 7, 1::2, d] = 0
    return pack(X, E, M)
def setup_inputs_corners(rng):
    fat = rng.random((N, 8, W)) < 0.5; X = cols(rng, counts(rng, fat), 255)
    E = lines(rng, fat, 0.1); M = rng.integers(0, 2, (N, 8, 16, A)); g, n = first(X)
    room = (0, 1, CAP - 1, CAP, CAP + 1, P, CAP, P - 1); even = np.arange(16)[:, None] % 2 == 0
    for q in range(N):
        for b in range(8):
            gg = g[q, b]; hot = np.flatnonzero((n[q, b] >= 9) & (gg != 0)); thin = np.flatnonzero(n[q, b] <= 8)
            c = int(rng.choice(np.array(room)))
            if q == 0: c = room[b]
            if q == N - 1: c = room[(b + 4) % 8]
            o = np.concatenate([np.array([P - 1]), rng.permutation(P - 1)]); yes = o[:c]; z = np.zeros((1, P), bool); z[0, o[c:]] = True
            e = np.where(rng.random((16, P)) < 0.2, (W - 1) * rng.integers(0, 2, (16, P)), rng.integers(0, W, (16, P)))
            m = (rng.random((16, P)) < rng.choice(np.array([0.0, 0.5, 1.0]), (1, P))).astype(np.int64)
            ge = gg[e]; m = np.where(even & z & (ge != 0), (ge > 0).astype(np.int64), m)
            e = np.where(~even & z, rng.choice(thin, (16, P)), e)
            k = 2 * rng.integers(0, 8, c); hh = rng.choice(hot, c); e[k, yes] = hh; m[k, yes] = (gg[hh] < 0).astype(np.int64)
            E[q, b, :, 0::S] = e; M[q, b, :, 0::S] = m
    return pack(X, E, M)
def setup_inputs_ties(rng):
    fat = rng.random((N, 8, W)) < 0.5
    n = np.where(fat, np.where(rng.random((N, 8, W)) < 0.8, 9, 16), 8); X = cols(rng, n, rng.choice(np.array([1, 2, 3]), (N, 8, 1, W)))
    E = lines(rng, fat, rng.choice(np.array([0.02, 0.2, 0.5]), (N, 8, 1, A)))
    E = np.take_along_axis(E, rng.integers(0, 3, (N, 8, 16, A)), 2)
    return pack(X, E, (rng.random((N, 8, 16, A)) < rng.choice(np.array([0.1, 0.5, 0.9]), (N, 8, 1, A))).astype(np.int64))
def setup_inputs_deep(rng):
    fat = rng.random((N, 8, W)) < 0.5; X = cols(rng, counts(rng, fat), 255)
    X[..., 0] = 0
    X[..., 3] = 253; X[..., hop(3, 64768 & (W - 1))] = 255
    X[..., 5] = 252; X[..., hop(5, 64512 & (W - 1))] = 255
    X[..., 7] = 255; X[..., hop(7, 65280 & (W - 1))] = 255; X[..., hop(7, 62976 & (W - 1))] = 255
    X[..., 11] = W >> 8
    X[..., W - 3] = top16(W - 21); X[..., hop(W - 3, W - 21)] = 0; X[..., hop(W - 3, W - 21) + 1] = 255
    X[..., 1001] = 255; X[..., 0, 1001] = 254; X[..., hop(1001, 65279 & (W - 1))] = 0
    X[..., 13] = 0; X[..., 7:, 13] = 255; X[..., hop(13, 52785 & (W - 1))] = 0
    X[..., 17] = 0; X[..., :9, 17] = 255; X[..., hop(17, 20655 & (W - 1))] = 0
    E = lines(rng, fat, 0.1); M = rng.integers(0, 2, (N, 8, 16, A)); s, n = first(X)
    h = hop(np.arange(W).reshape(1, 1, W), np.add.reduce(X * WT.reshape(1, 1, 16, 1), axis=2) & (W - 1))
    kind = np.argsort(rng.random((N, 8, P)), axis=-1) % 7
    for q in range(N):
        for b in range(8):
            if b in (1, 6):
                far = np.arange(W) >= (W >> 2); nn = n[q, b]; hh = h[q, b]
                thin = np.flatnonzero((nn <= 8) & far); hot = np.flatnonzero((nn >= 9) & (s[q, b] < 0) & (nn[hh] <= 8) & far[hh])
                E[q, b] = rng.choice(thin, (16, A))
                c = int(rng.integers(CAP >> 3, (CAP >> 2) + 1)); i = S * rng.permutation(P)[:c]; k = 2 * rng.integers(0, 8, c)
                E[q, b, k, i] = rng.choice(hot, c); M[q, b, k, i] = 1
                continue
            for v in range(1, 7):
                i = S * np.flatnonzero(kind[q, b] == v); k = 2 * rng.integers(0, 8, len(i))
                E[q, b, :, i] = 0; M[q, b, :, i] = 0
                if v == 1:
                    for w, e, m in ((0, 3, 1), (2, 3, 1), (4, 3, 1), (6, 5, 1), (7, 7, 1), (8, 7, 0), (9, 7, 1), (10, 7, 0), (11, 7, 1), (12, 7, 0), (13, 7, 0), (14, 7, 0)):
                        E[q, b, w, i] = e; M[q, b, w, i] = m
                elif v == 2:
                    E[q, b, k, i] = W - 3; M[q, b, k, i] = 1
                elif v == 3:
                    E[q, b, k, i] = 11; M[q, b, k, i] = 1; E[q, b, k + 1, i] = 7
                else:
                    E[q, b, k, i] = (1001, 13, 17)[v - 4]; M[q, b, k, i] = 1
    return pack(X, E, M)
def check_inputs(d):
    bad = []
    for k, lo, hi in (("xt", 0, 255), ("led", 0, W - 1), ("mk", 0, 1)):
        v = np.asarray(d[k]).astype(np.float64)
        if np.min(v) < lo or np.max(v) > hi or np.any(v != np.floor(v)): bad.append("range of " + k)
    return bad
def look(X, ix):
    return np.take_along_axis(X, ix.reshape(N, 8, 1, 16 * P), 3).reshape(N, 8, 16, 16, P)
def reference(xt, led, mk):
    X = xt.astype(np.float32).astype(np.int64).reshape(N, 8, 16, W)
    E = led.astype(np.int64).reshape(N, 8, 16, A); M = mk.astype(np.float32).astype(np.int64).reshape(N, 8, 16, A)
    kappa = np.zeros((N, 1, 1, 1), np.int64); ks = np.arange(16).reshape(1, 1, 16, 1)
    for t in range(RO):
        c = t % S; e = E[:, :, :, c::S].copy(); m = M[:, :, :, c::S].copy()
        x = look(X, e); q = x.copy(); b = np.zeros((N, 8, 16, P), np.int64)
        for k in range(16):
            mm = m[:, :, k][:, :, None, :]
            if k % 2 == 0: b = b + mm * x[:, :, :, k]
            else:
                q[:, :, :, k] = np.minimum(b, x[:, :, :, k]); b = b - mm * q[:, :, :, k]
        u = np.add.reduce(WT.reshape(1, 1, 16, 1, 1) * q, axis=2) & (W - 1)
        h = (((e * u) >> 5) + e + kappa) & (W - 1)
        g = np.add.reduce(np.sign(look(X, h) - q), axis=2); over = np.add.reduce((q > 0).astype(np.int64), axis=2)
        con = (over >= 9) & (((m == 1) & (g < 0)) | ((m == 0) & (g > 0)))
        best = np.argmax(np.where(con, np.abs(g), 0), axis=2)
        flip = np.any(con, axis=2)
        win = flip[:, :, None, :] & (ks == best[:, :, None, :])
        E[:, :, :, c::S] = np.where(win, h, e); M[:, :, :, c::S] = np.where(win, 1 - m, m)
        f = flip.astype(np.int64); kappa = (np.add.reduce(f.reshape(N, 8 * P), axis=1) & 31).reshape(N, 1, 1, 1)
        place = np.add.accumulate(f, axis=2) - 1; go = flip & (place < CAP)
        qb = np.take_along_axis(q, best[:, :, None, None, :], 3)[:, :, :, 0]; ub = np.take_along_axis(u, best[:, :, None, :], 2)[:, :, 0]
        new = X.copy()
        for r in range(N):
            d = (r + 1 + t % (N - 1)) % N
            for v in range(8):
                i = np.flatnonzero(go[r, v]); col = BL * place[r, v, i] + (ub[r, v, i] & (BL - 1))
                new[d, v][:, col] = (X[d, v][:, col] + qb[r, v][:, i]) >> 1
        X = new
    return {"yx": X.reshape(N, 128, W).astype(np.float32).astype(BF), "yl": E.reshape(N, 128, A).astype(np.float32), "ym": M.reshape(N, 128, A).astype(np.float32).astype(BF)}

@@ -1,0 +1,698 @@
+import numpy as np
+from concourse.bass import DstId, RemoteDMATransfer
+from concourse.mybir import dt, AluOpType, AxisListType, ActivationFunctionType
+
+ROUNDS = 4
+PRE = 2
+SW = 288
+TW = 8448
+SCRATCH = {
+    "TB": ("sbuf", [128, TW], "bfloat16"),
+    "LEDI": ("sbuf", [128, 16, 16, 2], "int32"), "MKI": ("sbuf", [128, 16, 16, 2], "bfloat16"),
+    "MS0": ("sbuf", [128, 16, 16], "float32"), "CB": ("sbuf", [128, 16, 16], "float32"), "OFFM": ("sbuf", [128, 256], "uint16"),
+    "OFFX": ("sbuf", [128, 64], "uint16"),
+    "EX": ("sbuf", [128, 16, 32], "float32"), "EY": ("sbuf", [128, 16, 32], "float32"),
+    "LL": ("sbuf", [128, 16, 16], "float32"), "M2": ("sbuf", [128, 256], "float32"),
+    "YLB": ("sbuf", [128, 512], "float32"), "YMB": ("sbuf", [128, 512], "bfloat16"),
+    "Q": ("sbuf", [128, 4096], "bfloat16"), "MX": ("sbuf", [128, 4096], "bfloat16"), "SB": ("sbuf", [128, 4096], "bfloat16"),
+    "D": ("sbuf", [128, 4096], "bfloat16"), "ZB": ("sbuf", [128, 4096], "bfloat16"), "DS": ("sbuf", [128, 4096], "bfloat16"),
+    "MM": ("sbuf", [128, 4096], "bfloat16"),
+    "UI": ("sbuf", [128, 256], "int32"), "UM": ("sbuf", [128, 256], "int32"), "PF": ("sbuf", [128, 256], "float32"),
+    "HI": ("sbuf", [128, 256], "int32"), "HH": ("sbuf", [128, 256], "int32"), "HO": ("sbuf", [128, 256], "uint16"),
+    "UL": ("sbuf", [128, 256], "int32"), "KA": ("sbuf", [128, 256], "float32"), "GG": ("sbuf", [128, 256], "float32"),
+    "KY": ("sbuf", [128, 256], "float32"), "RM": ("sbuf", [128, 256], "float32"),
+    "MI": ("sbuf", [128, 16], "int32"), "EB": ("sbuf", [128, 16], "int32"), "FL": ("sbuf", [128, 16], "bfloat16"),
+    "CU": ("sbuf", [128, 16], "bfloat16"), "IX": ("sbuf", [128, 16], "int32"), "IXU": ("sbuf", [128, 16], "uint16"),
+    "S2": ("sbuf", [128, 16], "int32"), "OU": ("sbuf", [128, 16], "uint16"),
+    "SM": ("sbuf", [128, 256], "int32"), "SH": ("sbuf", [128, 256], "int32"),
+    "WN": ("sbuf", [128, 256], "float32"), "W2": ("sbuf", [128, 256], "float32"), "DE": ("sbuf", [128, 256], "float32"),
+    "DW": ("sbuf", [128, 256], "float32"), "OW": ("sbuf", [128, 256], "float32"),
+    "K1": ("sbuf", [128, 8], "int32"), "K2": ("sbuf", [128, 8], "int32"), "K3": ("sbuf", [128, 8], "float32"),
+    "PI": ("sbuf", [128, 8], "int32"), "P4": ("sbuf", [128, 8], "int32"), "P15": ("sbuf", [128, 8], "int32"),
+    "PC": ("sbuf", [128, 8], "int32"), "PF1": ("sbuf", [128, 8], "float32"), "PG": ("sbuf", [128, 8], "float32"),
+    "PR": ("sbuf", [128, 8], "float32"), "PW": ("sbuf", [128, 8], "float32"), "PO": ("sbuf", [128, 8], "float32"),
+    "PE": ("sbuf", [128, 8], "float32"),
+    "IM": ("sbuf", [128, 128], "float32"), "IG": ("sbuf", [128, 128], "float32"), "IR": ("sbuf", [128, 16], "float32"),
+    "IC": ("sbuf", [128, 16], "int32"), "NBD": ("sbuf", [128, 128], "bfloat16"),
+    "EXM": ("sbuf", [128, 16, 32], "bfloat16"), "EYM": ("sbuf", [128, 16, 32], "bfloat16"),
+    "BD": ("sbuf", [128, 128], "bfloat16"), "IDN": ("sbuf", [128, 128], "bfloat16"), "NID": ("sbuf", [128, 128], "bfloat16"),
+    "I16": ("sbuf", [128, 128], "bfloat16"), "N256": ("sbuf", [128, 128], "bfloat16"), "ONE": ("sbuf", [128, 128], "bfloat16"),
+    "LB": ("sbuf", [128, 128], "bfloat16"), "CC": ("sbuf", [128, 16], "bfloat16"), "CF": ("sbuf", [128, 16], "bfloat16"),
+    "CW": ("sbuf", [128, 144], "bfloat16"), "UW": ("sbuf", [128, 144], "bfloat16"), "RMK": ("sbuf", [128, 16], "float32"),
+    "BR": ("sbuf", [128, 2048], "bfloat16"),
+    "KC": ("sbuf", [128, 256], "float32"), "BS": ("sbuf", [128, 16], "float32"), "FC": ("sbuf", [128, 16], "float32"),
+    "DC": ("sbuf", [128, 128], "bfloat16"), "KD": ("sbuf", [128, 256], "float32"), "CL": ("sbuf", [128, 16], "uint16"),
+    "ZZ": ("sbuf", [128, 16], "bfloat16"),
+    "XP": ("psum", [128, 2048], "float32"), "EP": ("psum", [128, 512], "float32"), "UP": ("psum", [128, 512], "float32"),
+    "ZP": ("psum", [128, 512], "float32"), "SP": ("psum", [128, 512], "float32"),
+}
+for _c in range(2):
+    SCRATCH["OFF%d" % _c] = ("sbuf", [128, 256], "uint16")
+    SCRATCH["E%d" % _c] = ("sbuf", [128, 256], "float32")
+    SCRATCH["SG%d" % _c] = ("sbuf", [128, 256], "float32")
+    SCRATCH["MB%d" % _c] = ("sbuf", [128, 256], "bfloat16")
+for _t in range(ROUNDS):
+    SCRATCH["SN%d" % _t] = ("sbuf", [128, SW], "bfloat16")
+    SCRATCH["LD%d" % _t] = ("sbuf", [128, SW], "bfloat16")
+SEMAPHORES = (["qV", "qS", "qP", "qG", "loc"] + ["d%d" % i for i in range(6)]
+              + ["%s%d" % (s, t) for s in ("arr", "hop") for t in range(ROUNDS)])
+
+
+def helpers(core, dst, topo):
+    if topo.may_write(core, dst):
+        return []
+    own = [c for c in topo.cores_of(core) if c != core and topo.may_write(c, dst)]
+    near = [c for c in own if topo.die(c) == topo.die(core)]
+    return (near or own)[:2]
+
+
+def target(rank, t, n):
+    return (rank + 1 + t % (n - 1)) % n
+
+
+def emask(engines):
+    m = 0
+    for e in engines:
+        m |= 1 << e
+    return m
+
+
+def parts_of(n):
+    w = SW // n
+    return [(i * w, (i + 1) * w) for i in range(n)]
+
+
+def bridge(g, core, T, topo):
+    n = len(T.cores)
+    sent = 0
+    for t in range(ROUNDS):
+        for r in range(n):
+            src, dst = T.cores[r], T.cores[target(r, t, n)]
+            hs = helpers(src, dst, topo)
+            if core not in hs:
+                continue
+            lo, hi = parts_of(len(hs))[hs.index(core)]
+            g.wait_ge(T.sem["hop%d" % t], len(topo.engines(src, core)) // len(hs))
+            rid, pid = topo.addr(dst, core)
+            piece = T["LD%d" % t][:, lo:hi]
+            g.remote_dma(piece, piece, T.sem["arr%d" % t], T.sem.loc, pid, rid, topo.mask(core, dst))
+            sent += len(topo.engines(core, dst))
+    if sent:
+        g.wait_ge(T.sem.loc, sent)
+
+
+def rank_program(g, core, T, topo):
+    rank = T.rank_of(core)
+    if rank is None:
+        bridge(g, core, T, topo)
+        return
+    A, F = AluOpType, ActivationFunctionType
+    n = len(T.cores)
+    Qs = {"V": g.vector, "S": g.scalar, "P": g.tensor, "G": g, "Y": g.sync}
+    seq = {"V": 0, "S": 0, "P": 0, "G": 0}
+    known = {q: {} for q in Qs}
+    log = {}
+    masks = {}
+
+    def a(name, *idx):
+        key = (name, str(idx))
+        if key not in masks:
+            shape = SCRATCH[name][1][1:]
+            bits = np.zeros(int(np.prod(shape)), np.uint8)
+            ids = np.arange(bits.size).reshape(shape)
+            bits[(ids[idx] if idx else ids).ravel()] = 1
+            exact = int.from_bytes(np.packbits(bits).tobytes(), "big")
+            bank = exact
+            if SCRATCH[name][0] == "psum":
+                wide = bits.copy()
+                for b in range(0, bits.size, 512):
+                    if bits[b:b + 512].any():
+                        wide[b:b + 512] = 1
+                bank = int.from_bytes(np.packbits(wide).tobytes(), "big")
+            masks[key] = (exact, bank)
+        return (name, T[name][(slice(None),) + tuple(idx)], masks[key][0], masks[key][1])
+
+    def c(name, lo, hi, step=1):
+        return a(name, slice(lo, hi, step) if step != 1 else slice(lo, hi))
+
+    def w(name):
+        return a(name)
+
+    def order(q, reads, writes):
+        need = {}
+        for isw, lst in ((False, reads), (True, writes)):
+            for name, _, ex, bk in lst:
+                psum = SCRATCH[name][0] == "psum"
+                for rq, src, cnt, rw, rex, rbk, clk in log.get(name, []):
+                    if psum and rq != q:
+                        hit = bk & rbk
+                    elif psum and q == "P":
+                        hit = 0
+                    else:
+                        hit = (isw or rw) and (ex & rex)
+                    if hit and need.get(src, (0, None))[0] < cnt:
+                        need[src] = (cnt, clk)
+        for src in sorted(need, key=lambda s: -len(need[s][1])):
+            cnt, clk = need[src]
+            if known[q].get(src, 0) < cnt:
+                Qs[q].wait_ge(T.sem[src], cnt)
+                for s, v in clk.items():
+                    known[q][s] = max(known[q].get(s, 0), v)
+                known[q][src] = max(known[q].get(src, 0), cnt)
+
+    def note(q, src, cnt, reads, writes, clk):
+        for isw, lst in ((False, reads), (True, writes)):
+            for name, _, ex, bk in lst:
+                old = log.get(name, [])
+                if isw:
+                    old = [x for x in old if x[4] & ~ex]
+                old.append((q, src, cnt, isw, ex, bk, clk))
+                log[name] = old
+
+    def run(q, fn, writes, reads):
+        order(q, reads, writes)
+        src = "q" + q
+        fn(Qs[q]).then_inc(T.sem[src], 1)
+        seq[q] += 1
+        clk = dict(known[q])
+        clk[src] = seq[q]
+        note(q, src, seq[q], reads, writes, clk)
+
+    def dma(q, sem, out, in_):
+        reads = [in_] if isinstance(in_, tuple) else []
+        writes = [out] if isinstance(out, tuple) else []
+        order(q, reads, writes)
+        Qs[q].dma_start(out[1] if writes else out, in_[1] if reads else in_).then_inc(T.sem[sem], 16)
+        note(q, sem, 16, reads, writes, dict(known[q]))
+
+    def ind(win, off):
+        return ("ind", win, off)
+
+    def opnd(x, reads):
+        if x[0] == "ind":
+            reads += [x[1], x[2]]
+            return x[1][1].indirect(x[2][1])
+        reads.append(x)
+        return x[1]
+
+    def sc(x, reads):
+        return opnd(x, reads) if isinstance(x, tuple) else x
+
+    def tt(out, in0, in1, op):
+        r = []
+        i0, i1 = opnd(in0, r), opnd(in1, r)
+        run("V", lambda e: e.tensor_tensor(out[1], i0, i1, op), [out], r)
+
+    def ts(out, in0, s1, op0, s2=None, op1=None):
+        r = []
+        i0, x1 = opnd(in0, r), sc(s1, r)
+        if op1 is None:
+            run("V", lambda e: e.tensor_scalar(out[1], i0, x1, None, op0), [out], r)
+        else:
+            x2 = sc(s2, r)
+            run("V", lambda e: e.tensor_scalar(out[1], i0, x1, x2, op0, op1), [out], r)
+
+    def cp(out, in_):
+        r = []
+        i0 = opnd(in_, r)
+        run("V", lambda e: e.tensor_copy(out[1], i0), [out], r)
+
+    def scatter(win, off, in_):
+        run("V", lambda e: e.tensor_copy(win[1].indirect(off[1]), in_[1]), [win], [in_, off])
+
+    def scan(out, d0, d1, op0, op1, initial=0.0):
+        run("V", lambda e: e.tensor_tensor_scan(out[1], d0[1], d1[1], initial, op0, op1), [out], [d0, d1])
+
+    def fill(out, v):
+        run("V", lambda e: e.memset(out[1], v), [out], [])
+
+    def turn(out, in_):
+        run("V", lambda e: e.transpose(out[1], in_[1]), [out], [in_])
+
+    def act(out, in_, func, scale=None, bias=None):
+        r = []
+        i0 = opnd(in_, r)
+        kw = {}
+        if scale is not None:
+            kw["scale"] = sc(scale, r)
+        if bias is not None:
+            kw["bias"] = sc(bias, r)
+        run("S", lambda e: e.activation(out[1], i0, func, **kw), [out], r)
+
+    def mm(out, lhsT, rhs, start=True, stop=True):
+        run("P", lambda e: e.matmul(out[1], lhsT[1], rhs[1], start, stop), [out], [lhsT, rhs])
+
+    def iota(out, pattern, base, cm, flag=True):
+        if flag:
+            run("G", lambda e: e.iota(out[1], pattern, base, cm, allow_small_or_imprecise_dtypes=True), [out], [])
+        else:
+            run("G", lambda e: e.iota(out[1], pattern, base, cm), [out], [])
+
+    dma("Y", "d0", w("LEDI"), T.led[:])
+    dma("S", "d1", w("MKI"), T.mk[:])
+    dma("Y", "d2", c("TB", 16, 2064), T.xt[:])
+
+    iota(c("PI", 0, 1), [[0, 1]], 0, 1, False)
+    iota(w("IG"), [[1, 8], [0, 16]], 0, 0)
+    iota(w("IR"), [[1, 16]], 0, 0)
+    iota(w("IM"), [[1, 128]], 0, 0)
+    iota(w("FC"), [[-16, 16]], 33024, 0)
+    iota(w("DC"), [[0, 64], [-4096, 2]], 4096, 0)
+    iota(w("CC"), [[1, 16]], 0, 0)
+    iota(w("KC"), [[0, 16], [-2048, 16]], 30720, 0)
+    iota(w("BS"), [[256, 16]], 240, 0)
+    iota(w("IC"), [[16, 16]], 15, 0, False)
+
+    ts(c("PC", 0, 1), c("PI", 0, 1), 4, A.arith_shift_right, 1, A.bitwise_and)
+    ts(c("P4", 0, 1), c("PI", 0, 1), 4, A.arith_shift_right)
+    ts(c("P15", 0, 1), c("PI", 0, 1), 15, A.bitwise_and)
+    cp(c("PO", 0, 1), c("PC", 0, 1))
+    ts(c("PE", 0, 1), c("PC", 0, 1), -1.0, A.mult, 1.0, A.add)
+    cp(c("PG", 0, 1), c("P4", 0, 1))
+    cp(c("PR", 0, 1), c("P15", 0, 1))
+    cp(c("PF1", 0, 1), c("PI", 0, 1))
+    ts(c("PW", 0, 1), c("P15", 0, 1), 2.0, A.mult, 1.0, A.add)
+    pg, pr, pp, pw = c("PG", 0, 1), c("PR", 0, 1), c("PF1", 0, 1), c("PW", 0, 1)
+    podd, peven = c("PO", 0, 1), c("PE", 0, 1)
+    ts(w("BD"), w("IG"), pg, A.is_equal)
+    ts(w("RMK"), w("IR"), pr, A.is_equal)
+    ts(w("NBD"), w("BD"), -1.0, A.mult)
+    ts(c("PE", 1, 2), peven, 256.0, A.mult)
+    ts(c("PO", 1, 2), podd, 256.0, A.mult)
+
+    def row_masks(lo, hi):
+        for r in range(lo, hi):
+            act(c("BR", 128 * r, 128 * r + 128), w("BD"), F.Copy, scale=c("RMK", r, r + 1))
+
+    row_masks(0, 8)
+    fill(c("TB", 0, 8), 0.0)
+    fill(c("TB", 8, 16), 4096.0)
+    ts(w("IDN"), w("IM"), pp, A.is_equal)
+    fill(w("CW"), 0.0)
+    ts(c("CW", 15, 143, 16), c("IG", 0, 128, 16), pg, A.is_equal)
+    ts(w("UW"), w("CW"), pw, A.mult)
+
+    ts(w("NID"), w("IDN"), -1.0, A.mult)
+    ts(w("I16"), w("IDN"), 16.0, A.mult)
+    fill(w("ONE"), 1.0)
+    fill(w("ZZ"), 0.0)
+    act(w("MS0"), a("MKI", slice(None), slice(None), 0), F.Copy, scale=4096.0)
+    fill(w("KD"), 1e9)
+    ts(c("KD", 0, 256, 16), w("FC"), pr, A.add)
+    run("G", lambda e: e.affine_select(w("LB")[1], w("NBD")[1], [[-1, 128]], A.is_ge, 0.0, 0, 1), [w("LB")], [w("NBD")])
+    iota(c("TB", 2064, TW), [[0, TW - 2064]], 0, 0)
+
+    def expand(src3, second, first="V"):
+        h0, h1 = slice(0, 16), slice(16, 32)
+        for h, eng, col in ((h0, first, peven), (h1, second, podd)):
+            if eng == "S":
+                act(a("EX", slice(None), h), src3, F.Copy, scale=col)
+            else:
+                ts(a("EX", slice(None), h), src3, col, A.mult)
+
+    def turned():
+        turn(w("EY"), w("EX"))
+        return a("EY", slice(None), slice(0, 16)), a("EY", slice(None), slice(16, 32))
+
+    def class_0():
+        tt(w("CB"), a("LEDI", slice(None), slice(None), 0), w("MS0"), A.add)
+        expand(w("CB"), "S")
+        h0, h1 = turned()
+        tt(w("LL"), h0, h1, A.add)
+        ts(w("OFFM"), w("LL"), -4080.0, A.add)
+        fill(c("OFFM", 15, 256, 16), 8)
+        ts(w("M2"), w("LL"), 4095.5, A.is_ge, -4096.0, A.mult)
+
+    def class_0_lines():
+        tt(w("E0"), w("LL"), w("M2"), A.add)
+        cp(w("OFF0"), w("E0"))
+
+    def marks_out(cl):
+        src = a("MKI", slice(None), slice(None), cl)
+        act(a("EXM", slice(None), slice(0, 16)), src, F.Copy, scale=c("PE", 1, 2))
+        act(a("EXM", slice(None), slice(16, 32)), src, F.Copy, scale=c("PO", 1, 2))
+
+    def marks_in(cl):
+        return [lambda: turn(w("EYM"), w("EXM")),
+                lambda: tt(w("MB%d" % cl), a("EYM", slice(None), slice(0, 16)), a("EYM", slice(None), slice(16, 32)), A.add),
+                lambda: act(w("SG%d" % cl), w("MB%d" % cl), F.Copy, scale=-512.0, bias=65536.0)]
+
+    def class_1_lines():
+        expand(a("LEDI", slice(None), slice(None), 1), "V")
+        h0, h1 = turned()
+        tt(w("E1"), h0, h1, A.add)
+        cp(w("OFF1"), w("E1"))
+
+    def masks_of(cl, pairs):
+        for i in pairs:
+            o = 512 * ((i + 2) % 4)
+            for k in (0, 1):
+                mm(c("XP", o + 256 * k, o + 256 * k + 256), c("BR", 128 * (2 * i + k), 128 * (2 * i + k) + 128), w("MB%d" % cl))
+            for k in (0, 1):
+                act(c("MM", 2 * i + k, 4096, 16), c("XP", o + 256 * k, o + 256 * k + 256), F.Copy)
+
+    def lines_to_psum(cl, first):
+        e = w("E%d" % cl)
+        act(c("EP", 0, 256), e, F.Copy)
+        if first:
+            act(c("EP", 256, 512), e, F.Copy, scale=32.0)
+        else:
+            act(c("EP", 256, 512), e, F.Identity, scale=32.0, bias=c("K3", 0, 1))
+
+    def items():
+        return c("TB", 16, 2064)
+
+    def quarter(name, q):
+        return c(name, 1024 * q, 1024 * q + 1024)
+
+    def lists(name, q):
+        return c(name, 64 * q, 64 * q + 64)
+
+    def gather_x(cl, q, eng):
+        src = ind(items(), lists("OFF%d" % cl, q))
+        if eng == "S":
+            act(quarter("Q", q), src, F.Copy)
+        else:
+            cp(quarter("Q", q), src)
+
+    def gather_mx(q, eng):
+        src = ind(c("TB", 0, 2064), lists("OFFM", q))
+        if eng == "S":
+            act(quarter("MX", q), src, F.Copy)
+        else:
+            cp(quarter("MX", q), src)
+
+    def lift(q):
+        for b in (2 * q, 2 * q + 1):
+            o = 512 * (b % 4)
+            mm(c("XP", o, o + 512), w("IDN"), c("Q", 512 * b, 512 * b + 512))
+
+    def fused_list(cl):
+        ts(w("OFFX"), lists("E%d" % cl, 1), 16.0, A.add)
+        fill(c("OFFX", 15, 64, 16), 8)
+
+    def marked_gather(q):
+        tt(quarter("MX", q), ind(c("TB", 0, 2064), w("OFFX")), quarter("MM", q), A.min)
+
+    def marked(q):
+        def one(k):
+            o = 256 * (k % 8)
+            return lambda: tt(c("MX", 256 * k, 256 * k + 240), c("XP", o, o + 240), c("MM", 256 * k, 256 * k + 240), A.min)
+        return [one(k) for k in range(4 * q, 4 * q + 4)]
+
+    def balances(h):
+        for r in range(16):
+            lo, hi = 2048 * h + r, 2048 * h + 2048
+            scan(c("SB", lo, hi, 16), c("MX", lo, hi, 16), w("DC"), A.subtract, A.min)
+
+    def odd_amounts(h):
+        for r in range(16):
+            lo, hi = 2048 * h + r, 2048 * h + 2048
+            tt(c("Q", lo + 16, hi, 32), c("XP", 16 + r, 2048, 32), c("SB", lo, hi, 32), A.min)
+
+    def sum_u(h, odd):
+        for r in range(16):
+            lo, hi = 2048 * h + r + 16 * odd, 2048 * h + 2048
+            mm(c("UP", 128 * h + odd, 128 * h + 128, 2), c("UW", 15 - r, 143 - r), c("Q", lo, hi, 32), r == 0, r == 15)
+
+    def count_over(q):
+        for r in range(16):
+            mm(lists("ZP", q), c("CW", 15 - r, 143 - r), c("ZB", 1024 * q + r, 1024 * q + 1024, 16), r == 0, r == 15)
+
+    def scores(q):
+        return c("SP", 64 * q, 64 * q + 64) if q < 2 else c("XP", 512 * (q - 2), 512 * (q - 2) + 64)
+
+    def score(q):
+        for r in range(16):
+            mm(scores(q), c("CW", 15 - r, 143 - r), c("DS", 1024 * q + r, 1024 * q + 1024, 16), r == 0, r == 15)
+
+    def weave(pattern, *steps):
+        its = [list(x) for x in steps]
+        for i in pattern:
+            its[i].pop(0)()
+        for x in its:
+            for f in x:
+                f()
+
+    def hashes(h):
+        s = (128 * h, 128 * h + 128)
+        return [lambda: cp(c("UI", *s), c("UP", *s)),
+                lambda: ts(c("UM", *s), c("UI", *s), 2047, A.bitwise_and),
+                lambda: tt(c("PF", *s), c("UM", *s), c("EP", *s), A.mult),
+                lambda: tt(c("HI", *s), c("PF", *s), c("EP", 256 + s[0], 256 + s[1]), A.add),
+                lambda: ts(c("HH", *s), c("HI", *s), 5, A.arith_shift_right, 2047, A.bitwise_and),
+                lambda: cp(c("HO", *s), c("HH", *s))]
+
+    def low_keys(h):
+        s = (128 * h, 128 * h + 128)
+        return [lambda: tt(c("KA", *s), c("UM", *s), c("SP", 256 + s[0], 256 + s[1]), A.add)]
+
+    def over(q, eng):
+        if eng == "S":
+            act(quarter("ZB", q), quarter("Q", q), F.Sign)
+        else:
+            ts(quarter("ZB", q), quarter("Q", q), 1.0, A.min)
+
+    def gate(lo, hi):
+        s = (lo, hi)
+        act(c("GG", *s), c("ZP", *s), F.Relu, scale=1048576.0, bias=-8388608.0)
+
+    def far(q):
+        act(quarter("D", q), ind(items(), lists("HO", q)), F.Copy)
+
+    def minus(b, out):
+        mm(out, w("IDN"), c("D", 512 * b, 512 * b + 512), True, False)
+        mm(out, w("NID"), c("Q", 512 * b, 512 * b + 512), False, True)
+
+    def sign_psum(b, src):
+        act(c("DS", 512 * b, 512 * b + 512), src, F.Sign)
+
+    def diff(q):
+        tt(quarter("D", q), ind(items(), lists("HO", q)), quarter("Q", q), A.subtract)
+
+    def sign(q, eng):
+        if eng == "S":
+            act(quarter("DS", q), quarter("D", q), F.Sign)
+        else:
+            ts(quarter("DS", q), quarter("D", q), 1.0, A.min, -1.0, A.max)
+
+    def keys(cl, p, lo, hi):
+        s = (lo, hi)
+        return [lambda: tt(p, p, c("SG%d" % cl, *s), A.mult),
+                lambda: tt(p, p, c("GG", *s), A.min),
+                lambda: tt(c("KY", *s), p, c("KA", *s), A.add),
+                lambda: scan(c("RM", *s), c("KD", *s), c("KY", *s), A.min, A.max, 1e9)]
+
+    def send(t):
+        dst = T.cores[target(rank, t, n)]
+        hs = helpers(core, dst, topo)
+        sn, ld = w("SN%d" % t), T["LD%d" % t]
+        order("G", [sn], [])
+        if not hs:
+            rid, pid = topo.addr(dst, core)
+            g.remote_dma(ld[:], sn[1], T.sem["arr%d" % t], T.sem.loc, pid, rid, topo.mask(core, dst))
+            return len(topo.engines(core, dst))
+        tr, cnt = [], 0
+        for i, (lo, hi) in enumerate(parts_of(len(hs))):
+            es = topo.engines(core, hs[i])
+            k = len(es) // len(hs)
+            rid, pid = topo.addr(hs[i], core)
+            tr.append(RemoteDMATransfer(dst_ids=[DstId(rid=rid, pnc=pid)], dma_engine_mask=emask(es[i * k:(i + 1) * k]),
+                                        remote_sem=T.sem["hop%d" % t], srcs=[T["SN%d" % t][:, lo:hi]], dsts=[ld[:, lo:hi]]))
+            cnt += k
+        g.remote_dma_fused(tr, local_sem=T.sem.loc)
+        return cnt
+
+    def winners(t):
+        best = c("RM", 15, 256, 16)
+        cp(w("MI"), best)
+        ts(w("FL"), best, 65535.5, A.is_ge)
+        ts(w("EB"), w("MI"), 7, A.arith_shift_right, 240, A.bitwise_and)
+        scan(w("CU"), w("FL"), w("ZZ"), A.add, A.max)
+        tt(w("IX"), w("BS"), w("EB"), A.subtract)
+        tt(w("CF"), w("FL"), w("CC"), A.mult)
+        cp(w("IXU"), w("IX"))
+        ts(w("S2"), w("MI"), 15, A.bitwise_and)
+        pl = c("ZP", 256, 272)
+        mm(pl, w("IDN"), w("CC"), True, False)
+        mm(pl, w("LB"), w("FL"), False, False)
+        mm(pl, w("N256"), w("FL"), False, False)
+        mm(pl, w("BD"), w("CU"), False, False)
+        mm(pl, w("NID"), w("CF"), False, True)
+        cp(c("SN%d" % t, 272, 288), w("S2"))
+        cp(c("SN%d" % t, 0, 256), ind(w("Q"), w("IXU")))
+        cp(c("SN%d" % t, 256, 272), pl)
+
+    def kappa():
+        mm(c("UP", 288, 289), w("ONE"), c("CU", 15, 16))
+        return [lambda: ts(c("K1", 0, 1), c("UP", 288, 289), 32.0, A.mult),
+                lambda: ts(c("K2", 0, 1), c("K1", 0, 1), 1023, A.bitwise_and),
+                lambda: cp(c("K3", 0, 1), c("K2", 0, 1))]
+
+    def moves():
+        tt(c("EP", 256, 512), w("HH"), c("EP", 0, 256), A.subtract)
+
+    def flips(cl, spread):
+        e, sg = w("E%d" % cl), w("SG%d" % cl)
+
+        def won():
+            tt(w("WN"), ind(w("RM"), w("CL")), w("KY"), A.is_equal)
+            if spread is not None:
+                masks_of(spread, range(PRE, 4))
+            act(c("ZP", 0, 256), w("WN"), F.Copy, scale=-2.0, bias=1.0)
+        return [won,
+                lambda: tt(w("DW"), c("EP", 256, 512), w("WN"), A.mult),
+                lambda: tt(e, c("EP", 0, 256), w("DW"), A.add),
+                lambda: tt(sg, c("ZP", 0, 256), sg, A.mult)]
+
+    def renew(cl):
+        cp(w("OFF%d" % cl), w("E%d" % cl))
+        act(w("MB%d" % cl), w("SG%d" % cl), F.Relu, scale=-1.0 / 256.0)
+        act(c("MB%d" % cl, 15, 256, 16), c("DC", 0, 32, 2), F.Copy)
+
+    def last(cl):
+        ts(w("DW"), w("SG%d" % cl), -1.0 / 64.0, A.mult, 1024.0, A.add)
+        tt(w("LL"), w("DW"), w("E%d" % cl), A.add)
+        expand(w("LL"), "V")
+        h0, h1 = turned()
+        tt(w("OW"), h0, h1, A.add)
+
+    def out_columns(cl):
+        m2 = w("M2")
+        ts(m2, w("OW"), 2047.5, A.is_ge, -2048.0, A.mult)
+        act(c("YMB", cl, 512, 2), m2, F.Copy, scale=-1.0 / 2048.0)
+        tt(c("YLB", cl, 512, 2), w("OW"), m2, A.add)
+
+    def apply(t):
+        src = T.cores[[r for r in range(n) if target(r, t, n) == rank][0]]
+        hs = helpers(src, core, topo)
+        ld = "LD%d" % t
+        note("R", "arr%d" % t, sum(len(topo.engines(h, core)) for h in (hs or [src])), [], [w(ld)], {})
+        of = c("UP", 272, 288)
+        mm(of, w("I16"), c(ld, 256, 272), True, False)
+        mm(of, w("IDN"), c(ld, 272, 288), False, True)
+        ts(w("OU"), of, 4096.0, A.add)
+        tt(w("SM"), ind(c("TB", 16, TW), w("OU")), c(ld, 0, 256), A.add)
+        ts(w("SH"), w("SM"), 1, A.arith_shift_right)
+        scatter(c("TB", 16, TW), w("OU"), w("SH"))
+
+    def first_half(cl):
+        for i in (0, 1):
+            act(c("Q", 512 * i, 512 * i + 512), ind(items(), c("OFF%d" % cl, 32 * i, 32 * i + 32)), F.Copy)
+        gather_x(cl, 1, "S")
+        marked_gather(1)
+        gather_x(cl, 2, "S")
+        gather_x(cl, 3, "S")
+        lift(0)
+        lift(1)
+        weave((), marked(0))
+        sum_u(0, 0)
+        balances(0)
+        odd_amounts(0)
+
+    def first_half_0():
+        gather_mx(0, "S")
+        class_0_lines()
+        gather_mx(1, "V")
+        gather_x(0, 0, "S")
+        balances(0)
+        gather_mx(2, "S")
+        gather_x(0, 1, "V")
+        gather_x(0, 2, "S")
+        lift(0)
+        lift(1)
+        ts(w("SG0"), w("M2"), 32.0, A.mult, 65536.0, A.add)
+        ts(w("N256"), w("IDN"), -256.0, A.mult)
+        ts(w("BS"), w("BS"), pr, A.add)
+        cp(w("CL"), w("IC"))
+        act(c("SP", 256, 512), w("KC"), F.Copy)
+        sum_u(0, 0)
+        gather_x(0, 3, "S")
+        lines_to_psum(0, True)
+        odd_amounts(0)
+        gather_mx(3, "V")
+
+    class_0()
+    total = 0
+    for t in range(ROUNDS):
+        cl, nx = t % 2, 1 - t % 2
+        bank = [c("XP", 512 * b, 512 * b + 512) for b in range(4)]
+        if t:
+            first_half(cl)
+        else:
+            first_half_0()
+        sum_u(0, 1)
+        lift(2)
+        over(0, "V")
+        over(1, "S")
+        if t:
+            weave((1, 1, 1, 0, 1), hashes(0), marked(2))
+            lift(3)
+            weave((), marked(3))
+        else:
+            marks_out(1)
+            row_masks(8, 16)
+            lift(3)
+            weave((), hashes(0))
+        count_over(0)
+        count_over(1)
+        sum_u(1, 0)
+        far(0)
+        gate(0, 128)
+        far(1)
+        balances(1)
+        odd_amounts(1)
+        sum_u(1, 1)
+        for b in range(4):
+            minus(b, bank[b])
+        over(2, "S")
+        weave((1, 0, 0, 2, 0, 2, 0), hashes(1), low_keys(0), marks_in(1) if t == 0 else [lambda: None] * 2)
+        for b in range(4):
+            sign_psum(b, bank[b])
+        diff(2)
+        count_over(2)
+        score(0)
+        score(1)
+        gate(128, 192)
+        sign(2, "S")
+        over(3, "S")
+        diff(3)
+        sign(3, "V")
+        if t == 0:
+            fill(c("MB1", 15, 256, 16), 4096.0)
+        score(2)
+        weave((0, 1, 0), keys(cl, c("SP", 0, 128), 0, 128), low_keys(1))
+        score(3)
+        count_over(3)
+        gate(192, 256)
+        if t + 1 < ROUNDS:
+            masks_of(nx, range(PRE))
+        weave((0, 0, 1, 0, 1, 0, 1, 1), keys(cl, scores(2), 128, 192), keys(cl, scores(3), 192, 256))
+        winners(t)
+        total += send(t)
+        moves()
+        if t == 0:
+            class_1_lines()
+        weave((1, 0, 1, 0, 1, 0, 1), *((kappa(), flips(cl, nx)) if t + 1 < ROUNDS else ([lambda: None] * 3, flips(cl, None))))
+        if t + 1 < ROUNDS:
+            masks_of(nx, range(4, 8))
+            lines_to_psum(nx, False)
+            fused_list(nx)
+        if t + 2 < ROUNDS:
+            renew(cl)
+        else:
+            last(cl)
+        if t + 2 == ROUNDS:
+            out_columns(cl)
+        apply(t)
+    dma("Y", "d5", T.yx[:], items())
+    out_columns(cl)
+    dma("S", "d3", T.ym[:], w("YMB"))
+    dma("S", "d4", T.yl[:], w("YLB"))
+    for d in ("d3", "d4", "d5"):
+        g.sync.wait_ge(T.sem[d], 16)
+    g.wait_ge(T.sem.loc, total)
+    for q in ("V", "S", "P", "G"):
+        g.wait_ge(T.sem["q" + q], seq[q])
+    for d in ("d0", "d1", "d2"):
+        g.wait_ge(T.sem[d], 16)

@@ -3,58 +3,68 @@ from concourse.bass import DstId, RemoteDMATransfer
 from concourse.mybir import dt, AluOpType, AxisListType, ActivationFunctionType
 
 ROUNDS = 4
-PRE = 2
 SW = 288
-TW = 8448
+TW = 4352
+NEG = 1408
+EARLY = 1024
+HEAD = 256
+TOP = 16777215
+FLOOR = -16384
+ORDER = """
+zS001 zV101 zS012 zS112 zS024 zS124
+r10 r00 s0 o00 r01 b0 e s1 r11 e q0 e b1 e o01 e q1 e f e y002 a02
+f o02 f o03 f r02 f g s2 f g f y024 a24 r03 g s3 r12 g o10 g r13 g o11 g y101 y112 m0 m1 n0 n1
+b2 b3 q2 q3 o12 o13 h h h h h h h n2 n3 t d2S d3V
+"""
+WAKE, GATHER, SCATTER, MATMUL, LOAD, HOP, ADD, SLACK, EAGER = 100, 1.25, 3.5, 0.6, 2400, 2000, 3000, 200, 30
 SCRATCH = {
-    "TB": ("sbuf", [128, TW], "bfloat16"),
-    "LEDI": ("sbuf", [128, 16, 16, 2], "int32"), "MKI": ("sbuf", [128, 16, 16, 2], "bfloat16"),
-    "MS0": ("sbuf", [128, 16, 16], "float32"), "CB": ("sbuf", [128, 16, 16], "float32"), "OFFM": ("sbuf", [128, 256], "uint16"),
-    "OFFX": ("sbuf", [128, 64], "uint16"),
-    "EX": ("sbuf", [128, 16, 32], "float32"), "EY": ("sbuf", [128, 16, 32], "float32"),
-    "LL": ("sbuf", [128, 16, 16], "float32"), "M2": ("sbuf", [128, 256], "float32"),
+    "TB": ("sbuf", [128, TW], "bfloat16"), "XH": ("sbuf", [128, TW], "float32"),
+    "LEDI": ("sbuf", [128, 512], "int32"), "MKI": ("sbuf", [128, 512], "bfloat16"), "EF": ("sbuf", [128, 256], "float32"),
     "YLB": ("sbuf", [128, 512], "float32"), "YMB": ("sbuf", [128, 512], "bfloat16"),
-    "Q": ("sbuf", [128, 4096], "bfloat16"), "MX": ("sbuf", [128, 4096], "bfloat16"), "SB": ("sbuf", [128, 4096], "bfloat16"),
+    "ZQ": ("sbuf", [128, 10240], "bfloat16"),
+    "MX": ("sbuf", [128, 4096], "bfloat16"), "SB": ("sbuf", [128, 4096], "bfloat16"), "DC": ("sbuf", [128, 2048], "bfloat16"),
     "D": ("sbuf", [128, 4096], "bfloat16"), "ZB": ("sbuf", [128, 4096], "bfloat16"), "DS": ("sbuf", [128, 4096], "bfloat16"),
-    "MM": ("sbuf", [128, 4096], "bfloat16"),
     "UI": ("sbuf", [128, 256], "int32"), "UM": ("sbuf", [128, 256], "int32"), "PF": ("sbuf", [128, 256], "float32"),
-    "HI": ("sbuf", [128, 256], "int32"), "HH": ("sbuf", [128, 256], "int32"), "HO": ("sbuf", [128, 256], "uint16"),
-    "UL": ("sbuf", [128, 256], "int32"), "KA": ("sbuf", [128, 256], "float32"), "GG": ("sbuf", [128, 256], "float32"),
-    "KY": ("sbuf", [128, 256], "float32"), "RM": ("sbuf", [128, 256], "float32"),
-    "MI": ("sbuf", [128, 16], "int32"), "EB": ("sbuf", [128, 16], "int32"), "FL": ("sbuf", [128, 16], "bfloat16"),
-    "CU": ("sbuf", [128, 16], "bfloat16"), "IX": ("sbuf", [128, 16], "int32"), "IXU": ("sbuf", [128, 16], "uint16"),
-    "S2": ("sbuf", [128, 16], "int32"), "OU": ("sbuf", [128, 16], "uint16"),
-    "SM": ("sbuf", [128, 256], "int32"), "SH": ("sbuf", [128, 256], "int32"),
-    "WN": ("sbuf", [128, 256], "float32"), "W2": ("sbuf", [128, 256], "float32"), "DE": ("sbuf", [128, 256], "float32"),
-    "DW": ("sbuf", [128, 256], "float32"), "OW": ("sbuf", [128, 256], "float32"),
+    "HI": ("sbuf", [128, 256], "int32"), "HH": ("sbuf", [128, 256], "int32"), "HS": ("sbuf", [128, 256], "float32"),
+    "HO": ("sbuf", [128, 256], "uint16"), "OFF": ("sbuf", [128, 256], "uint16"), "OF": ("sbuf", [128, 256], "float32"),
+    "KA": ("sbuf", [128, 256], "float32"), "GG": ("sbuf", [128, 256], "bfloat16"), "RM": ("sbuf", [128, 256], "float32"),
+    "KU": ("sbuf", [128, 256], "float32"), "RU": ("sbuf", [128, 256], "float32"),
+    "MI": ("sbuf", [128, 16], "int32"), "EB": ("sbuf", [128, 16], "int32"), "DU": ("sbuf", [128, 16], "int32"),
+    "FL": ("sbuf", [128, 16], "bfloat16"), "CU": ("sbuf", [128, 16], "bfloat16"),
+    "C255": ("sbuf", [128, 16], "bfloat16"), "N512": ("sbuf", [128, 128], "bfloat16"), "IX": ("sbuf", [128, 16], "int32"),
+    "IXU": ("sbuf", [128, 16], "uint16"), "S2": ("sbuf", [128, 16], "int32"), "OU": ("sbuf", [128, 16], "uint16"),
+    "KV": ("sbuf", [128, 16], "bfloat16"), "RX": ("sbuf", [128, 256], "bfloat16"),
+    "SH": ("sbuf", [128, 256], "int32"), "DE": ("sbuf", [128, 256], "float32"),
     "K1": ("sbuf", [128, 8], "int32"), "K2": ("sbuf", [128, 8], "int32"), "K3": ("sbuf", [128, 8], "float32"),
-    "PI": ("sbuf", [128, 8], "int32"), "P4": ("sbuf", [128, 8], "int32"), "P15": ("sbuf", [128, 8], "int32"),
-    "PC": ("sbuf", [128, 8], "int32"), "PF1": ("sbuf", [128, 8], "float32"), "PG": ("sbuf", [128, 8], "float32"),
-    "PR": ("sbuf", [128, 8], "float32"), "PW": ("sbuf", [128, 8], "float32"), "PO": ("sbuf", [128, 8], "float32"),
-    "PE": ("sbuf", [128, 8], "float32"),
-    "IM": ("sbuf", [128, 128], "float32"), "IG": ("sbuf", [128, 128], "float32"), "IR": ("sbuf", [128, 16], "float32"),
-    "IC": ("sbuf", [128, 16], "int32"), "NBD": ("sbuf", [128, 128], "bfloat16"),
-    "EXM": ("sbuf", [128, 16, 32], "bfloat16"), "EYM": ("sbuf", [128, 16, 32], "bfloat16"),
+    "PI": ("sbuf", [128, 8], "int32"), "PB": ("sbuf", [128, 8], "int32"), "PN": ("sbuf", [128, 8], "float32"),
+    "PD": ("sbuf", [128, 24], "float32"),
+    "IM": ("sbuf", [128, 144], "float32"), "IG": ("sbuf", [128, 128], "float32"), "I2": ("sbuf", [128, 16], "float32"),
+    "FA": ("sbuf", [128, 136], "float32"), "BA": ("sbuf", [128, 136], "float32"),
     "BD": ("sbuf", [128, 128], "bfloat16"), "IDN": ("sbuf", [128, 128], "bfloat16"), "NID": ("sbuf", [128, 128], "bfloat16"),
-    "I16": ("sbuf", [128, 128], "bfloat16"), "N256": ("sbuf", [128, 128], "bfloat16"), "ONE": ("sbuf", [128, 128], "bfloat16"),
-    "LB": ("sbuf", [128, 128], "bfloat16"), "CC": ("sbuf", [128, 16], "bfloat16"), "CF": ("sbuf", [128, 16], "bfloat16"),
-    "CW": ("sbuf", [128, 144], "bfloat16"), "UW": ("sbuf", [128, 144], "bfloat16"), "RMK": ("sbuf", [128, 16], "float32"),
-    "BR": ("sbuf", [128, 2048], "bfloat16"),
-    "KC": ("sbuf", [128, 256], "float32"), "BS": ("sbuf", [128, 16], "float32"), "FC": ("sbuf", [128, 16], "float32"),
-    "DC": ("sbuf", [128, 128], "bfloat16"), "KD": ("sbuf", [128, 256], "float32"), "CL": ("sbuf", [128, 16], "uint16"),
+    "I16": ("sbuf", [128, 128], "bfloat16"), "ONE": ("sbuf", [128, 128], "bfloat16"),
+    "C2": ("sbuf", [128, 128], "bfloat16"), "LT": ("sbuf", [128, 128], "bfloat16"),
+    "CW": ("sbuf", [128, 144], "bfloat16"), "UW": ("sbuf", [128, 144], "bfloat16"), "VW": ("sbuf", [128, 144], "bfloat16"),
+    "KC": ("sbuf", [128, 256], "bfloat16"), "KX": ("sbuf", [128, 256], "bfloat16"), "KR": ("sbuf", [128, 256], "bfloat16"),
+    "KD": ("sbuf", [128, 256], "float32"), "KE": ("sbuf", [128, 256], "float32"),
+    "I8K": ("sbuf", [128, 128], "bfloat16"), "IR": ("sbuf", [128, 128], "bfloat16"),
+    "RI": ("sbuf", [128, 256], "bfloat16"), "RK": ("sbuf", [128, 256], "bfloat16"), "CL": ("sbuf", [128, 16], "uint16"),
     "ZZ": ("sbuf", [128, 16], "bfloat16"),
-    "XP": ("psum", [128, 2048], "float32"), "EP": ("psum", [128, 512], "float32"), "UP": ("psum", [128, 512], "float32"),
-    "ZP": ("psum", [128, 512], "float32"), "SP": ("psum", [128, 512], "float32"),
+    "XP": ("psum", [128, 1024], "float32"), "KP": ("psum", [128, 512], "float32"), "UP": ("psum", [128, 512], "float32"),
+    "VP": ("psum", [128, 512], "float32"), "ZP": ("psum", [128, 512], "float32"), "EP": ("psum", [128, 512], "float32"),
+    "FP": ("psum", [128, 512], "float32"),
 }
 for _c in range(2):
-    SCRATCH["OFF%d" % _c] = ("sbuf", [128, 256], "uint16")
     SCRATCH["E%d" % _c] = ("sbuf", [128, 256], "float32")
     SCRATCH["SG%d" % _c] = ("sbuf", [128, 256], "float32")
-    SCRATCH["MB%d" % _c] = ("sbuf", [128, 256], "bfloat16")
+    SCRATCH["FA%d" % _c] = ("sbuf", [128, 136], "float32")
+    SCRATCH["FB%d" % _c] = ("sbuf", [128, 136], "bfloat16")
+    SCRATCH["BA%d" % _c] = ("sbuf", [128, 136], "float32")
+    SCRATCH["BH%d" % _c] = ("sbuf", [128, 128], "bfloat16")
+    SCRATCH["TS%d" % _c] = ("sbuf", [128, 144], "bfloat16")
 for _t in range(ROUNDS):
     SCRATCH["SN%d" % _t] = ("sbuf", [128, SW], "bfloat16")
     SCRATCH["LD%d" % _t] = ("sbuf", [128, SW], "bfloat16")
-SEMAPHORES = (["qV", "qS", "qP", "qG", "loc"] + ["d%d" % i for i in range(6)]
+SEMAPHORES = (["qV", "qS", "qP", "qG", "loc"] + ["d%d" % i for i in range(9)] + ["a%d" % i for i in range(4)]
               + ["%s%d" % (s, t) for s in ("arr", "hop") for t in range(ROUNDS)])
 
 
@@ -114,13 +124,11 @@ def rank_program(g, core, T, topo):
     log = {}
     masks = {}
 
-    def a(name, *idx):
-        key = (name, str(idx))
+    def c(name, lo, hi, step=1):
+        key = (name, lo, hi, step)
         if key not in masks:
-            shape = SCRATCH[name][1][1:]
-            bits = np.zeros(int(np.prod(shape)), np.uint8)
-            ids = np.arange(bits.size).reshape(shape)
-            bits[(ids[idx] if idx else ids).ravel()] = 1
+            bits = np.zeros(SCRATCH[name][1][1], np.uint8)
+            bits[lo:hi:step] = 1
             exact = int.from_bytes(np.packbits(bits).tobytes(), "big")
             bank = exact
             if SCRATCH[name][0] == "psum":
@@ -130,18 +138,16 @@ def rank_program(g, core, T, topo):
                         wide[b:b + 512] = 1
                 bank = int.from_bytes(np.packbits(wide).tobytes(), "big")
             masks[key] = (exact, bank)
-        return (name, T[name][(slice(None),) + tuple(idx)], masks[key][0], masks[key][1])
-
-    def c(name, lo, hi, step=1):
-        return a(name, slice(lo, hi, step) if step != 1 else slice(lo, hi))
+        ap = T[name][:, lo:hi:step] if step != 1 else T[name][:, lo:hi]
+        return (name, ap, masks[key][0], masks[key][1], len(range(lo, hi, step)))
 
     def w(name):
-        return a(name)
+        return c(name, 0, SCRATCH[name][1][1])
 
     def order(q, reads, writes):
         need = {}
         for isw, lst in ((False, reads), (True, writes)):
-            for name, _, ex, bk in lst:
+            for name, _, ex, bk, _n in lst:
                 psum = SCRATCH[name][0] == "psum"
                 for rq, src, cnt, rw, rex, rbk, clk in log.get(name, []):
                     if psum and rq != q:
@@ -162,28 +168,126 @@ def rank_program(g, core, T, topo):
 
     def note(q, src, cnt, reads, writes, clk):
         for isw, lst in ((False, reads), (True, writes)):
-            for name, _, ex, bk in lst:
+            for name, _, ex, bk, _n in lst:
                 old = log.get(name, [])
                 if isw:
                     old = [x for x in old if x[4] & ~ex]
                 old.append((q, src, cnt, isw, ex, bk, clk))
                 log[name] = old
 
-    def run(q, fn, writes, reads):
-        order(q, reads, writes)
-        src = "q" + q
-        fn(Qs[q]).then_inc(T.sem[src], 1)
-        seq[q] += 1
-        clk = dict(known[q])
-        clk[src] = seq[q]
-        note(q, src, seq[q], reads, writes, clk)
+    tasks, group, hold = [], [], []
 
-    def dma(q, sem, out, in_):
-        reads = [in_] if isinstance(in_, tuple) else []
+    fixed = []
+
+    def task(q, emit, writes, reads, cost, lag=0, adds=False, after=()):
+        if group:
+            x = group[0]
+            x["emit"].append(emit)
+            x["writes"] += writes
+            x["reads"] += reads
+            x["cost"] += cost
+            x["adds"] = adds
+            return x
+        tasks.append({"q": q, "emit": [emit], "writes": list(writes), "reads": list(reads), "cost": cost, "lag": lag,
+                      "adds": adds, "after": list(after) + hold, "fixed": q in fixed, "first": 0})
+        return tasks[-1]
+
+    def together(calls, first=0):
+        x = {"q": "P", "emit": [], "writes": [], "reads": [], "cost": 0, "lag": 0, "adds": False, "after": list(hold), "fixed": False,
+             "first": first}
+        tasks.append(x)
+        group.append(x)
+        for args in calls:
+            mm(*args)
+        group.pop()
+
+    def run(q, fn, writes, reads, cost, adds=False):
+        def emit():
+            order(q, reads, writes)
+            src = "q" + q
+            fn(Qs[q]).then_inc(T.sem[src], 1)
+            seq[q] += 1
+            clk = dict(known[q])
+            clk[src] = seq[q]
+            note(q, src, seq[q], reads, writes, clk)
+        task(q, emit, writes, reads, cost, 0, adds)
+
+    moved = {}
+
+    def dma(q, sem, out, in_, lag, add=False):
         writes = [out] if isinstance(out, tuple) else []
-        order(q, reads, writes)
-        Qs[q].dma_start(out[1] if writes else out, in_[1] if reads else in_).then_inc(T.sem[sem], 16)
-        note(q, sem, 16, reads, writes, dict(known[q]))
+        reads = ([in_] if isinstance(in_, tuple) else []) + (writes if add else [])
+
+        def emit():
+            order(q, reads, writes)
+            kw = {"accum_op": A.add} if add else {}
+            Qs[q].dma_start(out[1] if writes else out, in_[1] if reads else in_, **kw).then_inc(T.sem[sem], 16)
+            moved[sem] = moved.get(sem, 0) + 16
+            note(q, sem, moved[sem], reads, writes, dict(known[q]))
+        task(q, emit, writes, reads, 300 if add else 64, lag)
+
+    def links():
+        seen, last = {}, {}
+        for i, x in enumerate(tasks):
+            x["i"] = i
+            pre = set(y["i"] for y in x["after"])
+            for isw, lst in ((False, x["reads"]), (True, x["writes"])):
+                for a in lst:
+                    for j, wrote, ex, bk in seen.get(a[0], []):
+                        if isw and wrote and x["q"] == tasks[j]["q"] == "P":
+                            if bk & a[3] and not (x["adds"] and tasks[j]["adds"]):
+                                pre.add(j)
+                        elif (isw or wrote) and ex & a[2]:
+                            pre.add(j)
+            for isw, lst in ((False, x["reads"]), (True, x["writes"])):
+                for a in lst:
+                    old = seen.get(a[0], [])
+                    if isw and not x["adds"]:
+                        old = [y for y in old if y[2] & ~a[2]]
+                    seen[a[0]] = old + [(i, isw, a[2], a[3])]
+            pre.discard(i)
+            x["behind"] = None
+            if x["fixed"]:
+                if x["q"] in last and last[x["q"]] not in pre:
+                    x["behind"] = last[x["q"]]
+                    pre.add(x["behind"])
+                last[x["q"]] = i
+            x["pre"], x["post"] = pre, set()
+            for j in pre:
+                tasks[j]["post"].add(i)
+            x["banks"] = set((a[0], a[3]) for a in x["reads"] + x["writes"] if SCRATCH[a[0]][0] == "psum")
+
+    def issue():
+        links()
+        left = [len(x["pre"]) for x in tasks]
+        free, used, base = {}, {}, [0] * len(tasks)
+        ready = [x for x in tasks if not x["pre"]]
+        while ready:
+            at = {}
+            for x in ready:
+                t = max(free.get(x["q"], 0), base[x["i"]])
+                for name, bk in x["banks"]:
+                    for q, b, e in used.get(name, []):
+                        if q != x["q"] and b & bk:
+                            t = max(t, e + WAKE)
+                at[x["i"]] = t
+            q = min(ready, key=lambda y: (at[y["i"]], y["i"]))["q"]
+            mine = sorted([y for y in ready if y["q"] == q], key=lambda y: (-y["first"], y["i"]))
+            x = mine[0]
+            for y in mine[1:]:
+                if at[y["i"]] + EAGER < at[x["i"]] and at[y["i"]] + y["cost"] <= at[mine[0]["i"]] + (0 if mine[0]["first"] == 3 else SLACK):
+                    x = y
+            ready.remove(x)
+            free[q] = at[x["i"]] + x["cost"]
+            for name, bk in x["banks"]:
+                used[name] = [u for u in used.get(name, []) if not (u[0] == q and u[1] == bk)] + [(q, bk, free[q])]
+            for f in x["emit"]:
+                f()
+            for j in x["post"]:
+                base[j] = max(base[j], free[q] + x["lag"] + (0 if q == tasks[j]["q"] == "P" or tasks[j]["behind"] == x["i"] else WAKE))
+                left[j] -= 1
+                if not left[j]:
+                    ready.append(tasks[j])
 
     def ind(win, off):
         return ("ind", win, off)
@@ -198,36 +302,41 @@ def rank_program(g, core, T, topo):
     def sc(x, reads):
         return opnd(x, reads) if isinstance(x, tuple) else x
 
+    def cycles(out, ins, rate=None):
+        if ins and ins[0][0] == "ind":
+            return 70 + GATHER * out[4]
+        if rate is None:
+            rate = 0.5 if all(SCRATCH[x[0]][2] in ("bfloat16", "uint16") for x in [out] + ins) else 1
+        return max(64, rate * out[4])
+
     def tt(out, in0, in1, op):
         r = []
         i0, i1 = opnd(in0, r), opnd(in1, r)
-        run("V", lambda e: e.tensor_tensor(out[1], i0, i1, op), [out], r)
+        rate = 1 if "psum" in [SCRATCH[x[0]][0] for x in r] else 2
+        run("V", lambda e: e.tensor_tensor(out[1], i0, i1, op), [out], r, cycles(out, [in0, in1], rate))
 
     def ts(out, in0, s1, op0, s2=None, op1=None):
         r = []
         i0, x1 = opnd(in0, r), sc(s1, r)
         if op1 is None:
-            run("V", lambda e: e.tensor_scalar(out[1], i0, x1, None, op0), [out], r)
+            run("V", lambda e: e.tensor_scalar(out[1], i0, x1, None, op0), [out], r, cycles(out, [in0]))
         else:
             x2 = sc(s2, r)
-            run("V", lambda e: e.tensor_scalar(out[1], i0, x1, x2, op0, op1), [out], r)
+            run("V", lambda e: e.tensor_scalar(out[1], i0, x1, x2, op0, op1), [out], r, cycles(out, [in0]))
 
     def cp(out, in_):
         r = []
         i0 = opnd(in_, r)
-        run("V", lambda e: e.tensor_copy(out[1], i0), [out], r)
+        run("V", lambda e: e.tensor_copy(out[1], i0), [out], r, cycles(out, [in_]))
 
     def scatter(win, off, in_):
-        run("V", lambda e: e.tensor_copy(win[1].indirect(off[1]), in_[1]), [win], [in_, off])
+        run("V", lambda e: e.tensor_copy(win[1].indirect(off[1]), in_[1]), [win], [in_, off], 60 + SCATTER * in_[4])
 
     def scan(out, d0, d1, op0, op1, initial=0.0):
-        run("V", lambda e: e.tensor_tensor_scan(out[1], d0[1], d1[1], initial, op0, op1), [out], [d0, d1])
+        run("V", lambda e: e.tensor_tensor_scan(out[1], d0[1], d1[1], initial, op0, op1), [out], [d0, d1], cycles(out, [d0, d1]))
 
     def fill(out, v):
-        run("V", lambda e: e.memset(out[1], v), [out], [])
-
-    def turn(out, in_):
-        run("V", lambda e: e.transpose(out[1], in_[1]), [out], [in_])
+        run("V", lambda e: e.memset(out[1], v), [out], [], cycles(out, []))
 
     def act(out, in_, func, scale=None, bias=None):
         r = []
@@ -237,462 +346,423 @@ def rank_program(g, core, T, topo):
             kw["scale"] = sc(scale, r)
         if bias is not None:
             kw["bias"] = sc(bias, r)
-        run("S", lambda e: e.activation(out[1], i0, func, **kw), [out], r)
+        run("S", lambda e: e.activation(out[1], i0, func, **kw), [out], r, cycles(out, [in_], 1))
 
-    def mm(out, lhsT, rhs, start=True, stop=True):
-        run("P", lambda e: e.matmul(out[1], lhsT[1], rhs[1], start, stop), [out], [lhsT, rhs])
+    def mm(out, lhsT, rhs, start=True, stop=True, adds=False):
+        cost = MATMUL * max(64, out[4]) * (4 if SCRATCH[rhs[0]][2] == "float32" else 1)
+        run("P", lambda e: e.matmul(out[1], lhsT[1], rhs[1], start, stop), [out], [lhsT, rhs], cost, adds)
 
     def iota(out, pattern, base, cm, flag=True):
         if flag:
-            run("G", lambda e: e.iota(out[1], pattern, base, cm, allow_small_or_imprecise_dtypes=True), [out], [])
+            run("G", lambda e: e.iota(out[1], pattern, base, cm, allow_small_or_imprecise_dtypes=True), [out], [], 160 + 2 * out[4])
         else:
-            run("G", lambda e: e.iota(out[1], pattern, base, cm), [out], [])
+            run("G", lambda e: e.iota(out[1], pattern, base, cm), [out], [], 160 + 2 * out[4])
 
-    dma("Y", "d0", w("LEDI"), T.led[:])
-    dma("S", "d1", w("MKI"), T.mk[:])
-    dma("Y", "d2", c("TB", 16, 2064), T.xt[:])
+    dma("Y", "d0", c("LEDI", 0, HEAD), T.led[:, 0:HEAD], LOAD)
+    dma("S", "d1", c("MKI", 0, HEAD), T.mk[:, 0:HEAD], LOAD)
+    dma("Y", "d2", c("TB", 0, 1024), T.xt[:, 0:1024], LOAD + 600)
+    dma("S", "d6", c("TB", 1024, 2048), T.xt[:, 1024:2048], LOAD + 1200)
+    dma("Y", "d7", c("LEDI", HEAD, 512), T.led[:, HEAD:512], LOAD + 1800)
+    dma("S", "d8", c("MKI", HEAD, 512), T.mk[:, HEAD:512], LOAD + 1800)
 
     iota(c("PI", 0, 1), [[0, 1]], 0, 1, False)
-    iota(w("IG"), [[1, 8], [0, 16]], 0, 0)
-    iota(w("IR"), [[1, 16]], 0, 0)
-    iota(w("IM"), [[1, 128]], 0, 0)
-    iota(w("FC"), [[-16, 16]], 33024, 0)
-    iota(w("DC"), [[0, 64], [-4096, 2]], 4096, 0)
-    iota(w("CC"), [[1, 16]], 0, 0)
-    iota(w("KC"), [[0, 16], [-2048, 16]], 30720, 0)
-    iota(w("BS"), [[256, 16]], 240, 0)
-    iota(w("IC"), [[16, 16]], 15, 0, False)
+    iota(w("IM"), [[1, 144]], 0, 0)
+    iota(w("IG"), [[1, 16], [0, 8]], 0, 0)
+    iota(w("I2"), [[1, 2], [0, 8]], 0, 0)
+    iota(w("RI"), [[0, 2], [1, 16], [0, 8]], 0, 0)
+    for q in range(4):
+        if q < 2:
+            iota(c("DC", 1024 * q, 1024 * q + 1024), [[0, 512], [-4096, 2]], 4096, 0)
+        iota(c("ZQ", 4096 + 1024 * q, 5120 + 1024 * q, 2), [[0, 512]], -4096, 0)
+    iota(w("KC"), [[0, 16], [-16, 8], [-9, 2]], -7, 0)
+    iota(c("KX", 0, 256, 2), [[1, 128]], 0, 0)
+    iota(c("KX", 1, 256, 2), [[2, 128]], 1, 0)
+    iota(w("KR"), [[0, 128], [128, 2]], 128, 0)
+    for name, pattern, floor in (("KD", [[0, 16]], FLOOR), ("KE", [[-1, 16]], FLOOR + 15)):
+        iota(w(name), [[0, 256]], TOP, 0)
+        iota(c(name, 0, 256, 16), pattern, floor, 0)
 
-    ts(c("PC", 0, 1), c("PI", 0, 1), 4, A.arith_shift_right, 1, A.bitwise_and)
-    ts(c("P4", 0, 1), c("PI", 0, 1), 4, A.arith_shift_right)
-    ts(c("P15", 0, 1), c("PI", 0, 1), 15, A.bitwise_and)
-    cp(c("PO", 0, 1), c("PC", 0, 1))
-    ts(c("PE", 0, 1), c("PC", 0, 1), -1.0, A.mult, 1.0, A.add)
-    cp(c("PG", 0, 1), c("P4", 0, 1))
-    cp(c("PR", 0, 1), c("P15", 0, 1))
-    cp(c("PF1", 0, 1), c("PI", 0, 1))
-    ts(c("PW", 0, 1), c("P15", 0, 1), 2.0, A.mult, 1.0, A.add)
-    pg, pr, pp, pw = c("PG", 0, 1), c("PR", 0, 1), c("PF1", 0, 1), c("PW", 0, 1)
-    podd, peven = c("PO", 0, 1), c("PE", 0, 1)
-    ts(w("BD"), w("IG"), pg, A.is_equal)
-    ts(w("RMK"), w("IR"), pr, A.is_equal)
-    ts(w("NBD"), w("BD"), -1.0, A.mult)
-    ts(c("PE", 1, 2), peven, 256.0, A.mult)
-    ts(c("PO", 1, 2), podd, 256.0, A.mult)
+    fields = ((0, 127), (4, 7), (0, 15), (0, 1), (1, 7), (0, 7), (3, 1))
+    for i, (sh, mk) in enumerate(fields):
+        ts(c("PB", i, i + 1), c("PI", 0, 1), sh, A.arith_shift_right, mk, A.bitwise_and)
+    cp(c("PN", 0, 7), c("PB", 0, 7))
+    pp, pg, pr, podd, phalf, p7, phigh = [c("PN", i, i + 1) for i in range(7)]
+    col = [0]
 
-    def row_masks(lo, hi):
-        for r in range(lo, hi):
-            act(c("BR", 128 * r, 128 * r + 128), w("BD"), F.Copy, scale=c("RMK", r, r + 1))
+    def column(src, s1, op0, s2, op1):
+        out = c("PD", col[0], col[0] + 1)
+        col[0] += 1
+        ts(out, src, s1, op0, s2, op1)
+        return out
 
-    row_masks(0, 8)
-    fill(c("TB", 0, 8), 0.0)
-    fill(c("TB", 8, 16), 4096.0)
-    ts(w("IDN"), w("IM"), pp, A.is_equal)
-    fill(w("CW"), 0.0)
-    ts(c("CW", 15, 143, 16), c("IG", 0, 128, 16), pg, A.is_equal)
-    ts(w("UW"), w("CW"), pw, A.mult)
+    g16 = column(pg, 16.0, A.mult, 15.0, A.add)
+    peven = column(podd, -1.0, A.mult, 1.0, A.add)
+    fwd = column(phalf, g16, A.add, -7.0, A.add)
+    par_of = (peven, podd)
+    mneg = [column(x, -2048.0, A.mult, 0.0, A.add) for x in par_of]
+    ts(w("FA"), c("IM", 0, 136), fwd, A.is_equal)
+    for i in (0, 1):
+        act(w("FA%d" % i), w("FA"), F.Copy, scale=par_of[i])
+        act(w("FB%d" % i), w("FA"), F.Copy, scale=mneg[i])
+    pw = column(pr, 2.0, A.mult, 1.0, A.add)
+    p27 = column(p7, 2.0, A.mult, 0.0, A.add)
+    pv = column(p7, 2.0, A.mult, 1.0, A.add)
+    ts(w("CW"), w("IM"), g16, A.is_equal)
+    ts(w("IDN"), c("IM", 0, 128), pp, A.is_equal)
+    fill(w("C2"), 2048.0)
+    act(w("UW"), w("CW"), F.Copy, scale=pw)
+    act(w("VW"), w("CW"), F.Copy, scale=pv)
+    act(w("TS0"), w("CW"), F.Copy, scale=1048576.0)
+    act(w("TS1"), w("CW"), F.Copy, scale=-1048576.0)
+    act(w("NID"), w("IDN"), F.Copy, scale=-1.0)
 
-    ts(w("NID"), w("IDN"), -1.0, A.mult)
-    ts(w("I16"), w("IDN"), 16.0, A.mult)
-    fill(w("ONE"), 1.0)
-    fill(w("ZZ"), 0.0)
-    act(w("MS0"), a("MKI", slice(None), slice(None), 0), F.Copy, scale=4096.0)
-    fill(w("KD"), 1e9)
-    ts(c("KD", 0, 256, 16), w("FC"), pr, A.add)
-    run("G", lambda e: e.affine_select(w("LB")[1], w("NBD")[1], [[-1, 128]], A.is_ge, 0.0, 0, 1), [w("LB")], [w("NBD")])
-    iota(c("TB", 2064, TW), [[0, TW - 2064]], 0, 0)
+    later = {}
 
-    def expand(src3, second, first="V"):
-        h0, h1 = slice(0, 16), slice(16, 32)
-        for h, eng, col in ((h0, first, peven), (h1, second, podd)):
-            if eng == "S":
-                act(a("EX", slice(None), h), src3, F.Copy, scale=col)
-            else:
-                ts(a("EX", slice(None), h), src3, col, A.mult)
+    def more_constants():
+        won = [column(p27, -1.0, A.mult, 15.0 - i, A.add) for i in (0, 1)]
+        half = [column(pg, 2.0, A.mult, float(i), A.add) for i in (0, 1)]
+        bwd = column(p27, g16, A.add, -14.0, A.add)
+        plow = column(phigh, -1.0, A.mult, 1.0, A.add)
+        later.update(won=won, bwd=bwd, high=(plow, phigh))
+        for i in (0, 1):
+            ts(w("BH%d" % i), w("IG"), half[i], A.is_equal)
+        ts(w("CL"), w("I2"), p27, A.add)
+        ts(w("RK"), w("RI"), pr, A.is_equal)
+        fill(w("ONE"), 1.0)
+        fill(w("ZZ"), 0.0)
+        fill(w("C255"), 255.0)
+        act(w("N512"), w("IDN"), F.Copy, scale=-512.0)
+        tt(w("BD"), w("BH0"), w("BH1"), A.add)
+        act(w("I8K"), w("IDN"), F.Copy, scale=8192.0)
+        act(w("IR"), w("IDN"), F.Copy, scale=pr)
+        act(w("I16"), w("IDN"), F.Copy, scale=16.0)
+        run("G", lambda e: e.affine_select(w("LT")[1], w("BD")[1], [[1, 128]], A.is_gt, 0.0, 0, -1), [w("LT")], [w("BD")], 460)
 
-    def turned():
-        turn(w("EY"), w("EX"))
-        return a("EY", slice(None), slice(0, 16)), a("EY", slice(None), slice(16, 32))
+    def back_constants():
+        ts(w("BA"), c("IM", 0, 136), later["bwd"], A.is_equal)
+        for i in (0, 1):
+            act(w("BA%d" % i), w("BA"), F.Copy, scale=later["high"][i])
 
-    def class_0():
-        tt(w("CB"), a("LEDI", slice(None), slice(None), 0), w("MS0"), A.add)
-        expand(w("CB"), "S")
-        h0, h1 = turned()
-        tt(w("LL"), h0, h1, A.add)
-        ts(w("OFFM"), w("LL"), -4080.0, A.add)
-        fill(c("OFFM", 15, 256, 16), 8)
-        ts(w("M2"), w("LL"), 4095.5, A.is_ge, -4096.0, A.mult)
+    def to_lists(cl, outs, lo, hi, lines, marks, base=False):
+        for par, (name, at) in enumerate(outs):
+            o = c(name, at + 32 * lo, at + 32 * hi)
+            steps = [(w("IDN"), c("C2", 0, o[4]))] if base else []
+            for a1 in (0, 1):
+                if lines:
+                    steps.append((c("FA%d" % par, 8 - 8 * a1, 136 - 8 * a1), c("EF", 64 * lo + a1, 64 * hi, 2)))
+                if marks:
+                    steps.append((c("FB%d" % par, 8 - 8 * a1, 136 - 8 * a1), c("MKI", 128 * lo + cl + 2 * a1, 128 * hi, 4)))
+            together([(o, l, r, i == 0, i == len(steps) - 1) for i, (l, r) in enumerate(steps)])
 
-    def class_0_lines():
-        tt(w("E0"), w("LL"), w("M2"), A.add)
-        cp(w("OFF0"), w("E0"))
+    def to_rows(out, src):
+        for a1 in (0, 1):
+            together([(c(out, a1, 256, 2), c("BA%d" % a1, 1 - par, 129 - par), c(src, 128 * par, 128 * par + 128), par == 0, par == 1)
+                      for par in (0, 1)])
 
-    def marks_out(cl):
-        src = a("MKI", slice(None), slice(None), cl)
-        act(a("EXM", slice(None), slice(0, 16)), src, F.Copy, scale=c("PE", 1, 2))
-        act(a("EXM", slice(None), slice(16, 32)), src, F.Copy, scale=c("PO", 1, 2))
+    def first_lists(cl, parts):
+        outs = (("KP", 0), ("FP", 0))
+        for lo, hi in parts:
+            cp(c("EF", 64 * lo, 64 * hi), c("LEDI", 128 * lo + cl, 128 * hi, 2))
+            to_lists(cl, outs, lo, hi, True, True)
+            for par, (name, at) in enumerate(outs):
+                ts(lists("OFF", par, lo, hi), c(name, at + 32 * lo, at + 32 * hi), 2048.0, A.add)
+            to_lists(cl, (("EP", 256), ("EP", 384)), lo, hi, False, True, True)
+            to_lists(cl, (("EP", 0), ("EP", 128)), lo, hi, True, False)
 
-    def marks_in(cl):
-        return [lambda: turn(w("EYM"), w("EXM")),
-                lambda: tt(w("MB%d" % cl), a("EYM", slice(None), slice(0, 16)), a("EYM", slice(None), slice(16, 32)), A.add),
-                lambda: act(w("SG%d" % cl), w("MB%d" % cl), F.Copy, scale=-512.0, bias=65536.0)]
+    def first_signs(cl):
+        act(w("SG%d" % cl), c("EP", 256, 512), F.Copy, scale=-1.0 / 1024.0, bias=1.0)
 
-    def class_1_lines():
-        expand(a("LEDI", slice(None), slice(None), 1), "V")
-        h0, h1 = turned()
-        tt(w("E1"), h0, h1, A.add)
-        cp(w("OFF1"), w("E1"))
+    def first_lines(cl):
+        act(w("E%d" % cl), c("EP", 0, 256), F.Copy)
 
-    def masks_of(cl, pairs):
-        for i in pairs:
-            o = 512 * ((i + 2) % 4)
-            for k in (0, 1):
-                mm(c("XP", o + 256 * k, o + 256 * k + 256), c("BR", 128 * (2 * i + k), 128 * (2 * i + k) + 128), w("MB%d" % cl))
-            for k in (0, 1):
-                act(c("MM", 2 * i + k, 4096, 16), c("XP", o + 256 * k, o + 256 * k + 256), F.Copy)
+    def next_lists(cl):
+        act(c("EP", 256, 512), w("SG%d" % cl), F.Copy, scale=-1024.0, bias=1024.0)
+        tt(w("OF"), w("E%d" % cl), c("EP", 256, 512), A.add)
+        act(c("EP", 0, 256), w("E%d" % cl), F.Copy)
+        cp(w("OFF"), w("OF"))
 
-    def lines_to_psum(cl, first):
-        e = w("E%d" % cl)
-        act(c("EP", 0, 256), e, F.Copy)
+    def shifted(src, first):
         if first:
-            act(c("EP", 256, 512), e, F.Copy, scale=32.0)
+            act(c("FP", 0, 256), src, F.Copy, scale=32.0)
         else:
-            act(c("EP", 256, 512), e, F.Identity, scale=32.0, bias=c("K3", 0, 1))
+            act(c("FP", 0, 256), src, F.Identity, scale=32.0, bias=c("K3", 0, 1))
 
-    def items():
-        return c("TB", 16, 2064)
+    def outputs(cl):
+        to_rows("VP", "E%d" % cl)
+        to_rows("ZP", "SG%d" % cl)
+        act(c("YLB", cl, 512, 2), c("VP", 0, 256), F.Copy)
+        act(c("YMB", cl, 512, 2), c("ZP", 0, 256), F.Copy, scale=0.5, bias=0.5)
 
-    def quarter(name, q):
-        return c(name, 1024 * q, 1024 * q + 1024)
+    Z, ZE = 4096, 8192
 
-    def lists(name, q):
-        return c(name, 64 * q, 64 * q + 64)
+    def table():
+        return c("TB", 0, 4096)
 
-    def gather_x(cl, q, eng):
-        src = ind(items(), lists("OFF%d" % cl, q))
+    def lists(name, par, lo, hi):
+        return c(name, 128 * par + 32 * lo, 128 * par + 32 * hi)
+
+    def packed(name, par, lo, hi):
+        return c(name, 2048 * par + 512 * lo, 2048 * par + 512 * hi)
+
+    def amounts(par, lo, hi):
+        return c("ZQ", 1024 * lo + 1, 1024 * hi, 2) if par else c("ZQ", ZE + 512 * lo, ZE + 512 * hi)
+
+    def items(par, lo, hi):
+        return c("ZQ", Z + 1024 * lo + 1, Z + 1024 * hi, 2) if par else amounts(0, lo, hi)
+
+    def gather_z(eng, par, lo, hi):
+        out, src = items(par, lo, hi), ind(table(), lists("OFF", par, lo, hi))
         if eng == "S":
-            act(quarter("Q", q), src, F.Copy)
+            act(out, src, F.Copy)
         else:
-            cp(quarter("Q", q), src)
+            cp(out, src)
 
-    def gather_mx(q, eng):
-        src = ind(c("TB", 0, 2064), lists("OFFM", q))
-        if eng == "S":
-            act(quarter("MX", q), src, F.Copy)
-        else:
-            cp(quarter("MX", q), src)
+    def relu(par, q):
+        ts(c("MX", 1024 * q + par, 1024 * q + 1024, 2), items(par, q, q + 1), 0.0, A.max)
 
-    def lift(q):
-        for b in (2 * q, 2 * q + 1):
-            o = 512 * (b % 4)
-            mm(c("XP", o, o + 512), w("IDN"), c("Q", 512 * b, 512 * b + 512))
+    def restart(q):
+        ts(c("DC", 1024 * (q % 2), 1024 * (q % 2) + 1024, 16), c("ZQ", ZE + 512 * q, ZE + 512 * q + 512, 8), 0.0, A.max)
 
-    def fused_list(cl):
-        ts(w("OFFX"), lists("E%d" % cl, 1), 16.0, A.add)
-        fill(c("OFFX", 15, 64, 16), 8)
+    def balances(q):
+        scan(c("SB", 1024 * q, 1024 * q + 1024), c("MX", 1024 * q, 1024 * q + 1024),
+             c("DC", 1024 * (q % 2), 1024 * (q % 2) + 1024), A.subtract, A.min)
 
-    def marked_gather(q):
-        tt(quarter("MX", q), ind(c("TB", 0, 2064), w("OFFX")), quarter("MM", q), A.min)
+    def odd_amounts(q):
+        lo, hi = 1024 * q, 1024 * q + 1024
+        scan(c("ZQ", lo, hi), c("ZQ", Z + lo, Z + hi), c("SB", lo, hi), A.min, A.max)
 
-    def marked(q):
-        def one(k):
-            o = 256 * (k % 8)
-            return lambda: tt(c("MX", 256 * k, 256 * k + 240), c("XP", o, o + 240), c("MM", 256 * k, 256 * k + 240), A.min)
-        return [one(k) for k in range(4 * q, 4 * q + 4)]
+    def sum_u(par, lo, hi):
+        def cols(row):
+            if par:
+                return c("ZQ", 1024 * lo + 2 * row + 1, 1024 * hi, 32)
+            return c("ZQ", ZE + 512 * lo + row, ZE + 512 * hi, 16)
+        together([(lists("UP", par, lo, hi), c("UW", 15 - row, 143 - row), cols(row), row == 0, row == 15) for row in range(16)], 2)
 
-    def balances(h):
-        for r in range(16):
-            lo, hi = 2048 * h + r, 2048 * h + 2048
-            scan(c("SB", lo, hi, 16), c("MX", lo, hi, 16), w("DC"), A.subtract, A.min)
-
-    def odd_amounts(h):
-        for r in range(16):
-            lo, hi = 2048 * h + r, 2048 * h + 2048
-            tt(c("Q", lo + 16, hi, 32), c("XP", 16 + r, 2048, 32), c("SB", lo, hi, 32), A.min)
-
-    def sum_u(h, odd):
-        for r in range(16):
-            lo, hi = 2048 * h + r + 16 * odd, 2048 * h + 2048
-            mm(c("UP", 128 * h + odd, 128 * h + 128, 2), c("UW", 15 - r, 143 - r), c("Q", lo, hi, 32), r == 0, r == 15)
-
-    def count_over(q):
-        for r in range(16):
-            mm(lists("ZP", q), c("CW", 15 - r, 143 - r), c("ZB", 1024 * q + r, 1024 * q + 1024, 16), r == 0, r == 15)
-
-    def scores(q):
-        return c("SP", 64 * q, 64 * q + 64) if q < 2 else c("XP", 512 * (q - 2), 512 * (q - 2) + 64)
-
-    def score(q):
-        for r in range(16):
-            mm(scores(q), c("CW", 15 - r, 143 - r), c("DS", 1024 * q + r, 1024 * q + 1024, 16), r == 0, r == 15)
-
-    def weave(pattern, *steps):
-        its = [list(x) for x in steps]
-        for i in pattern:
-            its[i].pop(0)()
-        for x in its:
-            for f in x:
-                f()
-
-    def hashes(h):
-        s = (128 * h, 128 * h + 128)
-        return [lambda: cp(c("UI", *s), c("UP", *s)),
+    def hashes(cl, par, lo, hi):
+        s = (128 * par + 32 * lo, 128 * par + 32 * hi)
+        nm = c("EP", 256 + s[0], 256 + s[1])
+        return [lambda: (sum_u(par, lo, hi), tt(c("UI", *s), c("UP", *s), c("SG%d" % cl, *s), A.mult)),
                 lambda: ts(c("UM", *s), c("UI", *s), 2047, A.bitwise_and),
                 lambda: tt(c("PF", *s), c("UM", *s), c("EP", *s), A.mult),
-                lambda: tt(c("HI", *s), c("PF", *s), c("EP", 256 + s[0], 256 + s[1]), A.add),
+                lambda: tt(c("HI", *s), c("PF", *s), c("FP", *s), A.add),
                 lambda: ts(c("HH", *s), c("HI", *s), 5, A.arith_shift_right, 2047, A.bitwise_and),
-                lambda: cp(c("HO", *s), c("HH", *s))]
+                lambda: tt(c("HS", *s), c("HH", *s), nm, A.add if par else A.subtract),
+                lambda: ts(c("HO", *s), c("HS", *s), 0.0 if par else 2048.0, A.add)]
 
-    def low_keys(h):
-        s = (128 * h, 128 * h + 128)
-        return [lambda: tt(c("KA", *s), c("UM", *s), c("SP", 256 + s[0], 256 + s[1]), A.add)]
+    def sum_low(par, q):
+        def cols(row):
+            if par:
+                return c("ZQ", 256 * row + 1, 256 * row + 256, 2)
+            return c("ZQ", ZE + 128 * row, ZE + 128 * row + 128)
+        together([(c("VP", par, 256, 2), c("VW", 15 - row, 143 - row), cols(row), row == 0, row == 15)
+                  for row in range(4 * q, 4 * q + 4)], par)
 
-    def over(q, eng):
+    def over(par, q):
+        ts(packed("ZB", par, q, q + 1), amounts(par, q, q + 1), 0.0, A.not_equal)
+
+    def count_over(par, q):
+        at = 2048 * par
+        together([(c("ZP", par, 256, 2), c("CW", 15 - row, 143 - row), c("ZB", at + 128 * row, at + 128 * row + 128),
+                   row == 0, row == 15) for row in range(4 * q, 4 * q + 4)], par)
+
+    def open_keys():
+        together([(c("KP", 0, 256), w(l), w(r), l == "I8K", False) for l, r in (("I8K", "KC"), ("IDN", "KX"), ("IR", "KR"))])
+
+    def score(par, q):
+        at, last = 2048 * par, (par, q) == (1, 3)
+        together([(c("KP", par, 256, 2), c("TS%d" % par, 15 - row, 143 - row), c("DS", at + 128 * row, at + 128 * row + 128),
+                   False, last and row == 15, not last) for row in range(4 * q, 4 * q + 4)])
+
+    def gate():
+        act(w("KA"), c("VP", 0, 256), F.Abs)
+        act(w("GG"), c("ZP", 0, 256), F.Relu, scale=-33554432.0, bias=9 * 33554432.0)
+        mm(c("KP", 0, 256), w("NID"), w("GG"), False, False, True)
+
+    def far(par, lo, hi):
+        act(packed("D", par, lo, hi), ind(table(), lists("HO", par, lo, hi)), F.Copy)
+
+    def add_amounts(lo, hi):
+        dma("G", "a%d" % lo, packed("D", 0, lo, hi), amounts(0, lo, hi), ADD, True)
+        tasks[-1]["first"] = 3
+
+    def minus(q):
+        bank = c("XP", 512 * (q % 2), 512 * (q % 2) + 512)
+        together([(bank, w("NID"), amounts(1, q, q + 1), True, False), (bank, w("IDN"), packed("D", 1, q, q + 1), False, True)], 1)
+        act(packed("DS", 1, q, q + 1), bank, F.Sign)
+        score(1, q)
+
+    def sign(eng, par, q):
         if eng == "S":
-            act(quarter("ZB", q), quarter("Q", q), F.Sign)
+            act(packed("DS", par, q, q + 1), packed("D", par, q, q + 1), F.Sign)
         else:
-            ts(quarter("ZB", q), quarter("Q", q), 1.0, A.min)
+            ts(packed("DS", par, q, q + 1), packed("D", par, q, q + 1), 1.0, A.min, -1.0, A.max)
+        score(par, q)
 
-    def gate(lo, hi):
-        s = (lo, hi)
-        act(c("GG", *s), c("ZP", *s), F.Relu, scale=1048576.0, bias=-8388608.0)
+    def diff(q, eng):
+        tt(packed("D", 1, q, q + 1), ind(table(), lists("HO", 1, q, q + 1)), amounts(1, q, q + 1), A.subtract)
+        sign(eng, 1, q)
 
-    def far(q):
-        act(quarter("D", q), ind(items(), lists("HO", q)), F.Copy)
+    def halves(lo, hi):
+        act(c("XH", lo, hi), c("TB", lo, hi), F.Copy, scale=0.5, bias=-0.25)
 
-    def minus(b, out):
-        mm(out, w("IDN"), c("D", 512 * b, 512 * b + 512), True, False)
-        mm(out, w("NID"), c("Q", 512 * b, 512 * b + 512), False, True)
+    def negate(lo, hi):
+        cut = lo + (hi - lo) * NEG // 2048
+        ts(c("TB", 2048 + lo, 2048 + cut), c("TB", lo, cut), -1.0, A.mult)
+        act(c("TB", 2048 + cut, 2048 + hi), c("TB", cut, hi), F.Copy, scale=-1.0)
 
-    def sign_psum(b, src):
-        act(c("DS", 512 * b, 512 * b + 512), src, F.Sign)
+    def winners(t):
+        sn = "SN%d" % t
+        best = c("RM", 15, 256, 16)
+        scan(w("RM"), w("KD"), c("KP", 0, 256), A.min, A.max, float(TOP))
+        tt(w("KU"), c("KP", 0, 256), w("KA"), A.add)
+        cp(w("MI"), best)
+        ts(w("FL"), best, -0.5, A.is_ge)
+        ts(w("IX"), w("MI"), 16383, A.bitwise_and)
+        scan(w("CU"), w("FL"), w("ZZ"), A.add, A.max)
+        cp(w("IXU"), w("IX"))
+        act(c(sn, 0, 256), ind(w("ZQ"), w("IXU")), F.Abs, scale=0.5)
+        scan(w("RU"), w("KE"), w("KU"), A.min, A.max, float(TOP))
+        pl = c("UP", 288, 304)
+        together([(c("UP", 256, 257), w("LT"), c("CU", 15, 16)), (pl, w("IDN"), w("CU"), True, False),
+                  (pl, w("N512"), w("FL"), False, False), (pl, w("IDN"), w("C255"), False, True),
+                  (c("UP", 257, 258), w("ONE"), c("CU", 15, 16))])
+        tt(w("DU"), c("RU", 15, 256, 16), best, A.subtract)
+        ts(c(sn, 256, 272), pl, c("UP", 256, 257), A.add, pr, A.min)
+        ts(w("S2"), w("DU"), 15, A.bitwise_and)
+        cp(c(sn, 272, 288), w("S2"))
 
-    def diff(q):
-        tt(quarter("D", q), ind(items(), lists("HO", q)), quarter("Q", q), A.subtract)
-
-    def sign(q, eng):
-        if eng == "S":
-            act(quarter("DS", q), quarter("D", q), F.Sign)
-        else:
-            ts(quarter("DS", q), quarter("D", q), 1.0, A.min, -1.0, A.max)
-
-    def keys(cl, p, lo, hi):
-        s = (lo, hi)
-        return [lambda: tt(p, p, c("SG%d" % cl, *s), A.mult),
-                lambda: tt(p, p, c("GG", *s), A.min),
-                lambda: tt(c("KY", *s), p, c("KA", *s), A.add),
-                lambda: scan(c("RM", *s), c("KD", *s), c("KY", *s), A.min, A.max, 1e9)]
+    sent = [0]
 
     def send(t):
         dst = T.cores[target(rank, t, n)]
         hs = helpers(core, dst, topo)
         sn, ld = w("SN%d" % t), T["LD%d" % t]
-        order("G", [sn], [])
-        if not hs:
-            rid, pid = topo.addr(dst, core)
-            g.remote_dma(ld[:], sn[1], T.sem["arr%d" % t], T.sem.loc, pid, rid, topo.mask(core, dst))
-            return len(topo.engines(core, dst))
-        tr, cnt = [], 0
-        for i, (lo, hi) in enumerate(parts_of(len(hs))):
-            es = topo.engines(core, hs[i])
-            k = len(es) // len(hs)
-            rid, pid = topo.addr(hs[i], core)
-            tr.append(RemoteDMATransfer(dst_ids=[DstId(rid=rid, pnc=pid)], dma_engine_mask=emask(es[i * k:(i + 1) * k]),
-                                        remote_sem=T.sem["hop%d" % t], srcs=[T["SN%d" % t][:, lo:hi]], dsts=[ld[:, lo:hi]]))
-            cnt += k
-        g.remote_dma_fused(tr, local_sem=T.sem.loc)
-        return cnt
 
-    def winners(t):
-        best = c("RM", 15, 256, 16)
-        cp(w("MI"), best)
-        ts(w("FL"), best, 65535.5, A.is_ge)
-        ts(w("EB"), w("MI"), 7, A.arith_shift_right, 240, A.bitwise_and)
-        scan(w("CU"), w("FL"), w("ZZ"), A.add, A.max)
-        tt(w("IX"), w("BS"), w("EB"), A.subtract)
-        tt(w("CF"), w("FL"), w("CC"), A.mult)
-        cp(w("IXU"), w("IX"))
-        ts(w("S2"), w("MI"), 15, A.bitwise_and)
-        pl = c("ZP", 256, 272)
-        mm(pl, w("IDN"), w("CC"), True, False)
-        mm(pl, w("LB"), w("FL"), False, False)
-        mm(pl, w("N256"), w("FL"), False, False)
-        mm(pl, w("BD"), w("CU"), False, False)
-        mm(pl, w("NID"), w("CF"), False, True)
-        cp(c("SN%d" % t, 272, 288), w("S2"))
-        cp(c("SN%d" % t, 0, 256), ind(w("Q"), w("IXU")))
-        cp(c("SN%d" % t, 256, 272), pl)
+        def emit():
+            order("G", [sn], [])
+            if not hs:
+                rid, pid = topo.addr(dst, core)
+                g.remote_dma(ld[:], sn[1], T.sem["arr%d" % t], T.sem.loc, pid, rid, topo.mask(core, dst))
+                sent[0] += len(topo.engines(core, dst))
+                return
+            tr = []
+            for i, (lo, hi) in enumerate(parts_of(len(hs))):
+                es = topo.engines(core, hs[i])
+                k = len(es) // len(hs)
+                rid, pid = topo.addr(hs[i], core)
+                tr.append(RemoteDMATransfer(dst_ids=[DstId(rid=rid, pnc=pid)], dma_engine_mask=emask(es[i * k:(i + 1) * k]),
+                                            remote_sem=T.sem["hop%d" % t], srcs=[T["SN%d" % t][:, lo:hi]], dsts=[ld[:, lo:hi]]))
+                sent[0] += k
+            g.remote_dma_fused(tr, local_sem=T.sem.loc)
+        return task("G", emit, [], [sn], 200, HOP * (2 if hs else 1))
 
     def kappa():
-        mm(c("UP", 288, 289), w("ONE"), c("CU", 15, 16))
-        return [lambda: ts(c("K1", 0, 1), c("UP", 288, 289), 32.0, A.mult),
-                lambda: ts(c("K2", 0, 1), c("K1", 0, 1), 1023, A.bitwise_and),
-                lambda: cp(c("K3", 0, 1), c("K2", 0, 1))]
+        ts(c("K1", 0, 1), c("UP", 257, 258), 32.0, A.mult)
+        ts(c("K2", 0, 1), c("K1", 0, 1), 1023, A.bitwise_and)
+        cp(c("K3", 0, 1), c("K2", 0, 1))
 
     def moves():
-        tt(c("EP", 256, 512), w("HH"), c("EP", 0, 256), A.subtract)
+        tt(w("DE"), w("HH"), c("EP", 0, 256), A.subtract)
 
-    def flips(cl, spread):
+    def flips(cl):
         e, sg = w("E%d" % cl), w("SG%d" % cl)
+        ts(w("EB"), w("MI"), 16, A.arith_shift_right, 15, A.bitwise_and)
+        tt(w("KV"), w("EB"), c("UP", 288, 304), A.max)
+        tt(w("RX"), ind(w("KV"), w("CL")), w("RK"), A.mult)
+        together([(c("VP", 0, 128), w("BH%d" % a1), c("RX", 128 * a1, 128 * a1 + 128), a1 == 0, a1 == 1) for a1 in (0, 1)])
+        for par in (0, 1):
+            ts(c("XP", 128 * par, 128 * par + 128), c("VP", 0, 128), later["won"][par], A.is_equal)
+        act(c("ZP", 0, 256), c("XP", 0, 256), F.Copy, scale=-2.0, bias=1.0)
+        tt(c("XP", 512, 768), c("XP", 0, 256), w("DE"), A.mult)
+        tt(sg, c("ZP", 0, 256), sg, A.mult)
+        tt(e, c("XP", 512, 768), e, A.add)
 
-        def won():
-            tt(w("WN"), ind(w("RM"), w("CL")), w("KY"), A.is_equal)
-            if spread is not None:
-                masks_of(spread, range(PRE, 4))
-            act(c("ZP", 0, 256), w("WN"), F.Copy, scale=-2.0, bias=1.0)
-        return [won,
-                lambda: tt(w("DW"), c("EP", 256, 512), w("WN"), A.mult),
-                lambda: tt(e, c("EP", 0, 256), w("DW"), A.add),
-                lambda: tt(sg, c("ZP", 0, 256), sg, A.mult)]
-
-    def renew(cl):
-        cp(w("OFF%d" % cl), w("E%d" % cl))
-        act(w("MB%d" % cl), w("SG%d" % cl), F.Relu, scale=-1.0 / 256.0)
-        act(c("MB%d" % cl, 15, 256, 16), c("DC", 0, 32, 2), F.Copy)
-
-    def last(cl):
-        ts(w("DW"), w("SG%d" % cl), -1.0 / 64.0, A.mult, 1024.0, A.add)
-        tt(w("LL"), w("DW"), w("E%d" % cl), A.add)
-        expand(w("LL"), "V")
-        h0, h1 = turned()
-        tt(w("OW"), h0, h1, A.add)
-
-    def out_columns(cl):
-        m2 = w("M2")
-        ts(m2, w("OW"), 2047.5, A.is_ge, -2048.0, A.mult)
-        act(c("YMB", cl, 512, 2), m2, F.Copy, scale=-1.0 / 2048.0)
-        tt(c("YLB", cl, 512, 2), w("OW"), m2, A.add)
-
-    def apply(t):
+    def apply(t, own):
         src = T.cores[[r for r in range(n) if target(r, t, n) == rank][0]]
         hs = helpers(src, core, topo)
         ld = "LD%d" % t
-        note("R", "arr%d" % t, sum(len(topo.engines(h, core)) for h in (hs or [src])), [], [w(ld)], {})
+        count = sum(len(topo.engines(h, core)) for h in (hs or [src]))
+        task("R", lambda: note("R", "arr%d" % t, count, [], [w(ld)], {}), [w(ld)], [], 0, after=[own])
         of = c("UP", 272, 288)
-        mm(of, w("I16"), c(ld, 256, 272), True, False)
-        mm(of, w("IDN"), c(ld, 272, 288), False, True)
+        together([(of, w("I16"), c(ld, 256, 272), True, False), (of, w("IDN"), c(ld, 272, 288), False, True)], 2)
         ts(w("OU"), of, 4096.0, A.add)
-        tt(w("SM"), ind(c("TB", 16, TW), w("OU")), c(ld, 0, 256), A.add)
-        ts(w("SH"), w("SM"), 1, A.arith_shift_right)
-        scatter(c("TB", 16, TW), w("OU"), w("SH"))
+        tt(w("SH"), ind(w("XH"), w("OU")), c(ld, 0, 256), A.add)
+        scatter(w("TB"), w("OU"), w("SH"))
 
-    def first_half(cl):
-        for i in (0, 1):
-            act(c("Q", 512 * i, 512 * i + 512), ind(items(), c("OFF%d" % cl, 32 * i, 32 * i + 32)), F.Copy)
-        gather_x(cl, 1, "S")
-        marked_gather(1)
-        gather_x(cl, 2, "S")
-        gather_x(cl, 3, "S")
-        lift(0)
-        lift(1)
-        weave((), marked(0))
-        sum_u(0, 0)
-        balances(0)
-        odd_amounts(0)
-
-    def first_half_0():
-        gather_mx(0, "S")
-        class_0_lines()
-        gather_mx(1, "V")
-        gather_x(0, 0, "S")
-        balances(0)
-        gather_mx(2, "S")
-        gather_x(0, 1, "V")
-        gather_x(0, 2, "S")
-        lift(0)
-        lift(1)
-        ts(w("SG0"), w("M2"), 32.0, A.mult, 65536.0, A.add)
-        ts(w("N256"), w("IDN"), -256.0, A.mult)
-        ts(w("BS"), w("BS"), pr, A.add)
-        cp(w("CL"), w("IC"))
-        act(c("SP", 256, 512), w("KC"), F.Copy)
-        sum_u(0, 0)
-        gather_x(0, 3, "S")
-        lines_to_psum(0, True)
-        odd_amounts(0)
-        gather_mx(3, "V")
-
-    class_0()
-    total = 0
+    negate(0, 1024)
+    negate(1024, 2048)
+    first_lists(0, ((0, HEAD // 128), (HEAD // 128, 4)))
+    more_constants()
+    first_signs(0)
+    shifted(c("EP", 0, 256), True)
+    open_keys()
     for t in range(ROUNDS):
         cl, nx = t % 2, 1 - t % 2
-        bank = [c("XP", 512 * b, 512 * b + 512) for b in range(4)]
-        if t:
-            first_half(cl)
-        else:
-            first_half_0()
-        sum_u(0, 1)
-        lift(2)
-        over(0, "V")
-        over(1, "S")
-        if t:
-            weave((1, 1, 1, 0, 1), hashes(0), marked(2))
-            lift(3)
-            weave((), marked(3))
-        else:
-            marks_out(1)
-            row_masks(8, 16)
-            lift(3)
-            weave((), hashes(0))
-        count_over(0)
-        count_over(1)
-        sum_u(1, 0)
-        far(0)
-        gate(0, 128)
-        far(1)
-        balances(1)
-        odd_amounts(1)
-        sum_u(1, 1)
-        for b in range(4):
-            minus(b, bank[b])
-        over(2, "S")
-        weave((1, 0, 0, 2, 0, 2, 0), hashes(1), low_keys(0), marks_in(1) if t == 0 else [lambda: None] * 2)
-        for b in range(4):
-            sign_psum(b, bank[b])
-        diff(2)
-        count_over(2)
-        score(0)
-        score(1)
-        gate(128, 192)
-        sign(2, "S")
-        over(3, "S")
-        diff(3)
-        sign(3, "V")
-        if t == 0:
-            fill(c("MB1", 15, 256, 16), 4096.0)
-        score(2)
-        weave((0, 1, 0), keys(cl, c("SP", 0, 128), 0, 128), low_keys(1))
-        score(3)
-        count_over(3)
-        gate(192, 256)
-        if t + 1 < ROUNDS:
-            masks_of(nx, range(PRE))
-        weave((0, 0, 1, 0, 1, 0, 1, 1), keys(cl, scores(2), 128, 192), keys(cl, scores(3), 192, 256))
-        winners(t)
-        total += send(t)
+        chains = {"e": hashes(cl, 0, 0, 2), "f": hashes(cl, 0, 2, 4), "g": hashes(cl, 1, 0, 2), "h": hashes(cl, 1, 2, 4)}
+        steps = {"z": gather_z, "r": relu, "s": restart, "b": balances, "q": odd_amounts, "y": far, "a": add_amounts,
+                 "o": lambda par, q: (over(par, q), count_over(par, q), sum_low(par, q)),
+                 "m": minus, "t": gate, "d": diff, "n": lambda q: sign("S", 0, q)}
+        fixed.extend("VS")
+        for step in ORDER.split():
+            if step in chains:
+                chains[step].pop(0)()
+            else:
+                steps[step[0]](*[int(x) if x.isdigit() else x for x in step[1:]])
+        del fixed[:]
+        hold.append([x for x in tasks if x["q"] == "S"][-1])
         moves()
+        if 0 < t < ROUNDS - 1:
+            next_lists(nx)
+        for lo in range(0, EARLY, 256):
+            halves(lo, lo + 256)
+        hold.pop()
         if t == 0:
-            class_1_lines()
-        weave((1, 0, 1, 0, 1, 0, 1), *((kappa(), flips(cl, nx)) if t + 1 < ROUNDS else ([lambda: None] * 3, flips(cl, None))))
+            for lo in range(2048, TW, 384):
+                iota(c("XH", lo, lo + 384), [[0, 384]], 0, 0)
+        first = len(tasks)
+        fixed.append("V")
+        winners(t)
+        fixed.pop()
+        for x in tasks[first:]:
+            x["first"] = 3
+        hold.extend(tasks[-3:])
+        own = send(t)
         if t + 1 < ROUNDS:
-            masks_of(nx, range(4, 8))
-            lines_to_psum(nx, False)
-            fused_list(nx)
-        if t + 2 < ROUNDS:
-            renew(cl)
-        else:
-            last(cl)
-        if t + 2 == ROUNDS:
-            out_columns(cl)
-        apply(t)
-    dma("Y", "d5", T.yx[:], items())
-    out_columns(cl)
-    dma("S", "d3", T.ym[:], w("YMB"))
-    dma("S", "d4", T.yl[:], w("YLB"))
+            kappa()
+        for lo in range(EARLY, 2048, 256):
+            halves(lo, lo + 256)
+            tasks[-1]["first"] = -1
+        if t == 0:
+            first_lines(0)
+            first_lists(1, ((0, 4),))
+            first_signs(1)
+            shifted(c("EP", 0, 256), False)
+            first_lines(1)
+        elif t + 1 < ROUNDS:
+            shifted(w("E%d" % nx), False)
+        first = len(tasks)
+        apply(t, own)
+        if t + 1 < ROUNDS:
+            negate(0, 2048)
+        for x in tasks[first:]:
+            x["first"] = 3
+        flips(cl)
+        if t == 0:
+            back_constants()
+        if t + 2 >= ROUNDS:
+            outputs(cl)
+        if t + 1 < ROUNDS:
+            open_keys()
+        del hold[:]
+    dma("Y", "d5", T.yx[:], c("TB", 0, 2048), LOAD + 1200)
+    dma("S", "d3", T.ym[:], w("YMB"), LOAD)
+    dma("S", "d4", T.yl[:], w("YLB"), LOAD)
+    issue()
     for d in ("d3", "d4", "d5"):
         g.sync.wait_ge(T.sem[d], 16)
-    g.wait_ge(T.sem.loc, total)
+    g.wait_ge(T.sem.loc, sent[0])
     for q in ("V", "S", "P", "G"):
         g.wait_ge(T.sem["q" + q], seq[q])
-    for d in ("d0", "d1", "d2"):
-        g.wait_ge(T.sem[d], 16)
+    for d in moved:
+        if d not in ("d3", "d4", "d5"):
+            g.wait_ge(T.sem[d], moved[d])

@@ -8,15 +8,19 @@ TW = 4352
 NEG = 1408
 EARLY = 1024
 HEAD = 256
+LATE = 6
+HOPS, FIRST = 3000, 2000
+XT = 500
 TOP = 16777215
 FLOOR = -16384
 ORDER = """
-zS001 zV101 zS012 zS112 zS024 zS124
-r10 r00 s0 o00 r01 b0 e s1 r11 e q0 e b1 e o01 e q1 e f e y002 a02
-f o02 f o03 f r02 f g s2 f g f y024 a24 r03 g s3 r12 g o10 g r13 g o11 g y101 y112 m0 m1 n0 n1
-b2 b3 q2 q3 o12 o13 h h h h h h h n2 n3 t d2S d3V
+zS001 zV101 zS012 zS112 zS024 zS124 w00 u002
+r10 r00 o00 c00 w01 s0 r01 b0 e r11 e q0 k0 e b1 e o01 e u024 w02 w03 c01 q1 e f e y002 a02 u102 w10 w11 k1
+f o02 f o03 f r02 f g s2 f g f y024 a24 r03 g r12 g o10 g r13 g o11 g c02 c03 c10 c11 y101 y112
+b2 b3 m0 q2 w12 q3 u124 o12 o13 nV00 h h h h h h h j0 nS01 m1 c12 c13 w13 j1 nS02 nS03 t v
+p10 p00 p01 p11 p02 p03 x d2 iS20 d3 iV21 p12 nV13 p13 l0 l1
 """
-WAKE, GATHER, SCATTER, MATMUL, LOAD, HOP, ADD, SLACK, EAGER = 100, 1.25, 3.5, 0.6, 2400, 2000, 3000, 200, 30
+WAKE, GATHER, SCATTER, MATMUL, LOAD, HOP, ADD, SLACK, EAGER = 100, 1.25, 3.5, 0.6, 1800, 2000, 3000, 200, 30
 SCRATCH = {
     "TB": ("sbuf", [128, TW], "bfloat16"), "XH": ("sbuf", [128, TW], "float32"),
     "LEDI": ("sbuf", [128, 512], "int32"), "MKI": ("sbuf", [128, 512], "bfloat16"), "EF": ("sbuf", [128, 256], "float32"),
@@ -26,13 +30,14 @@ SCRATCH = {
     "D": ("sbuf", [128, 4096], "bfloat16"), "ZB": ("sbuf", [128, 4096], "bfloat16"), "DS": ("sbuf", [128, 4096], "bfloat16"),
     "UI": ("sbuf", [128, 256], "int32"), "UM": ("sbuf", [128, 256], "int32"), "PF": ("sbuf", [128, 256], "float32"),
     "HI": ("sbuf", [128, 256], "int32"), "HH": ("sbuf", [128, 256], "int32"), "HS": ("sbuf", [128, 256], "float32"),
-    "HO": ("sbuf", [128, 256], "uint16"), "OFF": ("sbuf", [128, 256], "uint16"), "OF": ("sbuf", [128, 256], "float32"),
+    "HO": ("sbuf", [128, 256], "uint16"), "OFF": ("sbuf", [128, 256], "uint16"),
+    "IDF": ("sbuf", [128, 128], "float32"), "NDF": ("sbuf", [128, 128], "float32"),
     "KA": ("sbuf", [128, 256], "float32"), "GG": ("sbuf", [128, 256], "bfloat16"), "RM": ("sbuf", [128, 256], "float32"),
     "KU": ("sbuf", [128, 256], "float32"), "RU": ("sbuf", [128, 256], "float32"),
-    "MI": ("sbuf", [128, 16], "int32"), "EB": ("sbuf", [128, 16], "int32"), "DU": ("sbuf", [128, 16], "int32"),
+    "MI": ("sbuf", [128, 16], "int32"), "EB": ("sbuf", [128, 16], "int32"), "KI": ("sbuf", [128, 256], "int32"),
     "FL": ("sbuf", [128, 16], "bfloat16"), "CU": ("sbuf", [128, 16], "bfloat16"),
     "C255": ("sbuf", [128, 16], "bfloat16"), "N512": ("sbuf", [128, 128], "bfloat16"), "IX": ("sbuf", [128, 16], "int32"),
-    "IXU": ("sbuf", [128, 16], "uint16"), "S2": ("sbuf", [128, 16], "int32"), "OU": ("sbuf", [128, 16], "uint16"),
+    "IXU": ("sbuf", [128, 16], "uint16"), "KL": ("sbuf", [128, 256], "int32"), "OU": ("sbuf", [128, 16], "uint16"),
     "KV": ("sbuf", [128, 16], "bfloat16"), "RX": ("sbuf", [128, 256], "bfloat16"),
     "SH": ("sbuf", [128, 256], "int32"), "DE": ("sbuf", [128, 256], "float32"),
     "K1": ("sbuf", [128, 8], "int32"), "K2": ("sbuf", [128, 8], "int32"), "K3": ("sbuf", [128, 8], "float32"),
@@ -59,13 +64,14 @@ for _c in range(2):
     SCRATCH["FA%d" % _c] = ("sbuf", [128, 136], "float32")
     SCRATCH["FB%d" % _c] = ("sbuf", [128, 136], "bfloat16")
     SCRATCH["BA%d" % _c] = ("sbuf", [128, 136], "float32")
+    SCRATCH["BB%d" % _c] = ("sbuf", [128, 136], "bfloat16")
     SCRATCH["BH%d" % _c] = ("sbuf", [128, 128], "bfloat16")
     SCRATCH["TS%d" % _c] = ("sbuf", [128, 144], "bfloat16")
 for _t in range(ROUNDS):
     SCRATCH["SN%d" % _t] = ("sbuf", [128, SW], "bfloat16")
     SCRATCH["LD%d" % _t] = ("sbuf", [128, SW], "bfloat16")
-SEMAPHORES = (["qV", "qS", "qP", "qG", "loc"] + ["d%d" % i for i in range(9)] + ["a%d" % i for i in range(4)]
-              + ["%s%d" % (s, t) for s in ("arr", "hop") for t in range(ROUNDS)])
+SEMAPHORES = (["qV", "qS", "qP", "qG", "loc"] + ["d%d" % i for i in range(10)] + ["a%d" % i for i in range(4)]
+              + ["%s%d" % (s, t) for s in ("arr0_", "arr1_", "hop") for t in range(ROUNDS)])
 
 
 def helpers(core, dst, topo):
@@ -80,16 +86,9 @@ def target(rank, t, n):
     return (rank + 1 + t % (n - 1)) % n
 
 
-def emask(engines):
-    m = 0
-    for e in engines:
-        m |= 1 << e
-    return m
-
-
 def parts_of(n):
-    w = SW // n
-    return [(i * w, (i + 1) * w) for i in range(n)]
+    cuts = [0] + [SW * i // n // 32 * 32 + 32 for i in range(1, n)] + [SW]
+    return list(zip(cuts, cuts[1:]))
 
 
 def bridge(g, core, T, topo):
@@ -102,10 +101,10 @@ def bridge(g, core, T, topo):
             if core not in hs:
                 continue
             lo, hi = parts_of(len(hs))[hs.index(core)]
-            g.wait_ge(T.sem["hop%d" % t], len(topo.engines(src, core)) // len(hs))
+            g.wait_ge(T.sem["hop%d" % t], len(topo.engines(src, core)))
             rid, pid = topo.addr(dst, core)
             piece = T["LD%d" % t][:, lo:hi]
-            g.remote_dma(piece, piece, T.sem["arr%d" % t], T.sem.loc, pid, rid, topo.mask(core, dst))
+            g.remote_dma(piece, piece, T.sem["arr%d_%d" % (hs.index(core), t)], T.sem.loc, pid, rid, topo.mask(core, dst))
             sent += len(topo.engines(core, dst))
     if sent:
         g.wait_ge(T.sem.loc, sent)
@@ -193,8 +192,8 @@ def rank_program(g, core, T, topo):
         return tasks[-1]
 
     def together(calls, first=0):
-        x = {"q": "P", "emit": [], "writes": [], "reads": [], "cost": 0, "lag": 0, "adds": False, "after": list(hold), "fixed": False,
-             "first": first}
+        x = {"q": "P", "emit": [], "writes": [], "reads": [], "cost": 0, "lag": 0, "adds": False, "after": list(hold),
+             "fixed": "P" in fixed, "first": first}
         tasks.append(x)
         group.append(x)
         for args in calls:
@@ -360,24 +359,24 @@ def rank_program(g, core, T, topo):
 
     dma("Y", "d0", c("LEDI", 0, HEAD), T.led[:, 0:HEAD], LOAD)
     dma("S", "d1", c("MKI", 0, HEAD), T.mk[:, 0:HEAD], LOAD)
-    dma("Y", "d2", c("TB", 0, 1024), T.xt[:, 0:1024], LOAD + 600)
-    dma("S", "d6", c("TB", 1024, 2048), T.xt[:, 1024:2048], LOAD + 1200)
-    dma("Y", "d7", c("LEDI", HEAD, 512), T.led[:, HEAD:512], LOAD + 1800)
-    dma("S", "d8", c("MKI", HEAD, 512), T.mk[:, HEAD:512], LOAD + 1800)
+    dma("Y", "d2", c("TB", 0, 1024), T.xt[:, 0:1024], LOAD + XT)
+    dma("S", "d6", c("TB", 1024, 2048), T.xt[:, 1024:2048], LOAD + 2 * XT)
+    dma("Y", "d7", c("LEDI", HEAD, 512), T.led[:, HEAD:512], LOAD + 3 * XT)
+    dma("S", "d8", c("MKI", HEAD, 512), T.mk[:, HEAD:512], LOAD + 3 * XT)
 
     iota(c("PI", 0, 1), [[0, 1]], 0, 1, False)
     iota(w("IM"), [[1, 144]], 0, 0)
-    iota(w("IG"), [[1, 16], [0, 8]], 0, 0)
-    iota(w("I2"), [[1, 2], [0, 8]], 0, 0)
-    iota(w("RI"), [[0, 2], [1, 16], [0, 8]], 0, 0)
+    iota(c("DC", 0, 1024), [[0, 512], [-4096, 2]], 4096, 0)
+    dma("Y", "d9", c("DC", 1024, 2048), c("DC", 0, 1024), LOAD)
     for q in range(4):
-        if q < 2:
-            iota(c("DC", 1024 * q, 1024 * q + 1024), [[0, 512], [-4096, 2]], 4096, 0)
         iota(c("ZQ", 4096 + 1024 * q, 5120 + 1024 * q, 2), [[0, 512]], -4096, 0)
     iota(w("KC"), [[0, 16], [-16, 8], [-9, 2]], -7, 0)
     iota(c("KX", 0, 256, 2), [[1, 128]], 0, 0)
     iota(c("KX", 1, 256, 2), [[2, 128]], 1, 0)
     iota(w("KR"), [[0, 128], [128, 2]], 128, 0)
+    iota(w("IG"), [[1, 16], [0, 8]], 0, 0)
+    iota(w("I2"), [[1, 2], [0, 8]], 0, 0)
+    iota(w("RI"), [[0, 2], [1, 16], [0, 8]], 0, 0)
     for name, pattern, floor in (("KD", [[0, 16]], FLOOR), ("KE", [[-1, 16]], FLOOR + 15)):
         iota(w(name), [[0, 256]], TOP, 0)
         iota(c(name, 0, 256, 16), pattern, floor, 0)
@@ -412,9 +411,6 @@ def rank_program(g, core, T, topo):
     fill(w("C2"), 2048.0)
     act(w("UW"), w("CW"), F.Copy, scale=pw)
     act(w("VW"), w("CW"), F.Copy, scale=pv)
-    act(w("TS0"), w("CW"), F.Copy, scale=1048576.0)
-    act(w("TS1"), w("CW"), F.Copy, scale=-1048576.0)
-    act(w("NID"), w("IDN"), F.Copy, scale=-1.0)
 
     later = {}
 
@@ -424,24 +420,35 @@ def rank_program(g, core, T, topo):
         bwd = column(p27, g16, A.add, -14.0, A.add)
         plow = column(phigh, -1.0, A.mult, 1.0, A.add)
         later.update(won=won, bwd=bwd, high=(plow, phigh))
-        for i in (0, 1):
-            ts(w("BH%d" % i), w("IG"), half[i], A.is_equal)
-        ts(w("CL"), w("I2"), p27, A.add)
-        ts(w("RK"), w("RI"), pr, A.is_equal)
+        later.update(half=half)
+        ts(w("NID"), w("IDN"), -1.0, A.mult)
+        ts(w("I8K"), w("IDN"), 8192.0, A.mult)
+        ts(w("IR"), w("IDN"), pr, A.mult)
+        ts(w("TS0"), w("CW"), 1048576.0, A.mult)
+        ts(w("TS1"), w("CW"), -1048576.0, A.mult)
+        ts(w("N512"), w("IDN"), -512.0, A.mult)
+        ts(w("I16"), w("IDN"), 16.0, A.mult)
         fill(w("ONE"), 1.0)
         fill(w("ZZ"), 0.0)
         fill(w("C255"), 255.0)
-        act(w("N512"), w("IDN"), F.Copy, scale=-512.0)
+
+    def group_constants():
+        for i in (0, 1):
+            ts(w("BH%d" % i), w("IG"), later["half"][i], A.is_equal)
         tt(w("BD"), w("BH0"), w("BH1"), A.add)
-        act(w("I8K"), w("IDN"), F.Copy, scale=8192.0)
-        act(w("IR"), w("IDN"), F.Copy, scale=pr)
-        act(w("I16"), w("IDN"), F.Copy, scale=16.0)
         run("G", lambda e: e.affine_select(w("LT")[1], w("BD")[1], [[1, 128]], A.is_gt, 0.0, 0, -1), [w("LT")], [w("BD")], 460)
 
+    def spread_constants():
+        ts(w("CL"), w("I2"), p27, A.add)
+        ts(w("RK"), w("RI"), pr, A.is_equal)
+
     def back_constants():
+        act(w("IDF"), w("IDN"), F.Copy)
+        act(w("NDF"), w("IDN"), F.Copy, scale=-1024.0)
         ts(w("BA"), c("IM", 0, 136), later["bwd"], A.is_equal)
         for i in (0, 1):
             act(w("BA%d" % i), w("BA"), F.Copy, scale=later["high"][i])
+            act(w("BB%d" % i), w("BA"), F.Copy, scale=later["high"][i])
 
     def to_lists(cl, outs, lo, hi, lines, marks, base=False):
         for par, (name, at) in enumerate(outs):
@@ -454,9 +461,9 @@ def rank_program(g, core, T, topo):
                     steps.append((c("FB%d" % par, 8 - 8 * a1, 136 - 8 * a1), c("MKI", 128 * lo + cl + 2 * a1, 128 * hi, 4)))
             together([(o, l, r, i == 0, i == len(steps) - 1) for i, (l, r) in enumerate(steps)])
 
-    def to_rows(out, src):
+    def to_rows(out, src, by):
         for a1 in (0, 1):
-            together([(c(out, a1, 256, 2), c("BA%d" % a1, 1 - par, 129 - par), c(src, 128 * par, 128 * par + 128), par == 0, par == 1)
+            together([(c(out, a1, 256, 2), c(by % a1, 1 - par, 129 - par), c(src, 128 * par, 128 * par + 128), par == 0, par == 1)
                       for par in (0, 1)])
 
     def first_lists(cl, parts):
@@ -477,9 +484,10 @@ def rank_program(g, core, T, topo):
 
     def next_lists(cl):
         act(c("EP", 256, 512), w("SG%d" % cl), F.Copy, scale=-1024.0, bias=1024.0)
-        tt(w("OF"), w("E%d" % cl), c("EP", 256, 512), A.add)
         act(c("EP", 0, 256), w("E%d" % cl), F.Copy)
-        cp(w("OFF"), w("OF"))
+        o = c("FP", 256, 512)
+        together([(o, w("IDF"), w("E%d" % cl), True, False), (o, w("NDF"), w("SG%d" % cl), False, True)])
+        ts(w("OFF"), o, 1024.0, A.add)
 
     def shifted(src, first):
         if first:
@@ -488,10 +496,11 @@ def rank_program(g, core, T, topo):
             act(c("FP", 0, 256), src, F.Identity, scale=32.0, bias=c("K3", 0, 1))
 
     def outputs(cl):
-        to_rows("VP", "E%d" % cl)
-        to_rows("ZP", "SG%d" % cl)
+        to_rows("VP", "E%d" % cl, "BA%d")
+        act(w("GG"), w("SG%d" % cl), F.Copy, scale=0.5, bias=0.5)
+        to_rows("ZP", "GG", "BB%d")
         act(c("YLB", cl, 512, 2), c("VP", 0, 256), F.Copy)
-        act(c("YMB", cl, 512, 2), c("ZP", 0, 256), F.Copy, scale=0.5, bias=0.5)
+        act(c("YMB", cl, 512, 2), c("ZP", 0, 256), F.Copy)
 
     Z, ZE = 4096, 8192
 
@@ -521,7 +530,7 @@ def rank_program(g, core, T, topo):
         ts(c("MX", 1024 * q + par, 1024 * q + 1024, 2), items(par, q, q + 1), 0.0, A.max)
 
     def restart(q):
-        ts(c("DC", 1024 * (q % 2), 1024 * (q % 2) + 1024, 16), c("ZQ", ZE + 512 * q, ZE + 512 * q + 512, 8), 0.0, A.max)
+        ts(c("DC", 0, 2048, 16), c("ZQ", ZE + 512 * q, ZE + 512 * q + 1024, 8), 0.0, A.max)
 
     def balances(q):
         scan(c("SB", 1024 * q, 1024 * q + 1024), c("MX", 1024 * q, 1024 * q + 1024),
@@ -541,7 +550,7 @@ def rank_program(g, core, T, topo):
     def hashes(cl, par, lo, hi):
         s = (128 * par + 32 * lo, 128 * par + 32 * hi)
         nm = c("EP", 256 + s[0], 256 + s[1])
-        return [lambda: (sum_u(par, lo, hi), tt(c("UI", *s), c("UP", *s), c("SG%d" % cl, *s), A.mult)),
+        return [lambda: tt(c("UI", *s), c("UP", *s), c("SG%d" % cl, *s), A.mult),
                 lambda: ts(c("UM", *s), c("UI", *s), 2047, A.bitwise_and),
                 lambda: tt(c("PF", *s), c("UM", *s), c("EP", *s), A.mult),
                 lambda: tt(c("HI", *s), c("PF", *s), c("FP", *s), A.add),
@@ -574,8 +583,9 @@ def rank_program(g, core, T, topo):
                    False, last and row == 15, not last) for row in range(4 * q, 4 * q + 4)])
 
     def gate():
-        act(w("KA"), c("VP", 0, 256), F.Abs)
         act(w("GG"), c("ZP", 0, 256), F.Relu, scale=-33554432.0, bias=9 * 33554432.0)
+
+    def add_gate():
         mm(c("KP", 0, 256), w("NID"), w("GG"), False, False, True)
 
     def far(par, lo, hi):
@@ -585,22 +595,33 @@ def rank_program(g, core, T, topo):
         dma("G", "a%d" % lo, packed("D", 0, lo, hi), amounts(0, lo, hi), ADD, True)
         tasks[-1]["first"] = 3
 
+    def bank(q):
+        return c("XP", 512 * q, 512 * q + 512)
+
     def minus(q):
-        bank = c("XP", 512 * (q % 2), 512 * (q % 2) + 512)
-        together([(bank, w("NID"), amounts(1, q, q + 1), True, False), (bank, w("IDN"), packed("D", 1, q, q + 1), False, True)], 1)
-        act(packed("DS", 1, q, q + 1), bank, F.Sign)
-        score(1, q)
+        mm(bank(q), w("NID"), amounts(1, q, q + 1), True, False)
+
+    def plus(q):
+        mm(bank(q), w("IDN"), packed("D", 1, q, q + 1), False, True)
+
+    def sign_bank(q):
+        act(packed("DS", 1, q, q + 1), bank(q), F.Sign)
 
     def sign(eng, par, q):
         if eng == "S":
             act(packed("DS", par, q, q + 1), packed("D", par, q, q + 1), F.Sign)
         else:
             ts(packed("DS", par, q, q + 1), packed("D", par, q, q + 1), 1.0, A.min, -1.0, A.max)
-        score(par, q)
 
-    def diff(q, eng):
+    def sign_half(eng, q, h):
+        lo = 2048 + 512 * q + 256 * h
+        if eng == "S":
+            act(c("DS", lo, lo + 256), c("D", lo, lo + 256), F.Sign)
+        else:
+            ts(c("DS", lo, lo + 256), c("D", lo, lo + 256), 1.0, A.min, -1.0, A.max)
+
+    def diff(q):
         tt(packed("D", 1, q, q + 1), ind(table(), lists("HO", 1, q, q + 1)), amounts(1, q, q + 1), A.subtract)
-        sign(eng, 1, q)
 
     def halves(lo, hi):
         act(c("XH", lo, hi), c("TB", lo, hi), F.Copy, scale=0.5, bias=-0.25)
@@ -610,51 +631,54 @@ def rank_program(g, core, T, topo):
         ts(c("TB", 2048 + lo, 2048 + cut), c("TB", lo, cut), -1.0, A.mult)
         act(c("TB", 2048 + cut, 2048 + hi), c("TB", cut, hi), F.Copy, scale=-1.0)
 
-    def winners(t):
+    def low_abs():
+        act(w("KA"), c("VP", 0, 256), F.Abs)
+
+    def low_bits(i):
+        if i:
+            ts(w("KL"), w("KI"), 15, A.bitwise_and)
+        else:
+            cp(w("KI"), w("KA"))
+
+    def winners(t, parts):
         sn = "SN%d" % t
         best = c("RM", 15, 256, 16)
         scan(w("RM"), w("KD"), c("KP", 0, 256), A.min, A.max, float(TOP))
-        tt(w("KU"), c("KP", 0, 256), w("KA"), A.add)
+        tt(w("KU"), c("KP", 0, 256), w("KL"), A.add)
         cp(w("MI"), best)
         ts(w("FL"), best, -0.5, A.is_ge)
         ts(w("IX"), w("MI"), 16383, A.bitwise_and)
         scan(w("CU"), w("FL"), w("ZZ"), A.add, A.max)
         cp(w("IXU"), w("IX"))
-        act(c(sn, 0, 256), ind(w("ZQ"), w("IXU")), F.Abs, scale=0.5)
+        for lo, hi in parts:
+            lo = max(lo, 32)
+            act(c(sn, lo, hi), ind(w("ZQ"), c("IXU", lo // 16 - 2, hi // 16 - 2)), F.Abs, scale=0.5)
         scan(w("RU"), w("KE"), w("KU"), A.min, A.max, float(TOP))
         pl = c("UP", 288, 304)
         together([(c("UP", 256, 257), w("LT"), c("CU", 15, 16)), (pl, w("IDN"), w("CU"), True, False),
                   (pl, w("N512"), w("FL"), False, False), (pl, w("IDN"), w("C255"), False, True),
                   (c("UP", 257, 258), w("ONE"), c("CU", 15, 16))])
-        tt(w("DU"), c("RU", 15, 256, 16), best, A.subtract)
-        ts(c(sn, 256, 272), pl, c("UP", 256, 257), A.add, pr, A.min)
-        ts(w("S2"), w("DU"), 15, A.bitwise_and)
-        cp(c(sn, 272, 288), w("S2"))
+        ts(c(sn, 0, 16), pl, c("UP", 256, 257), A.add, pr, A.min)
+        tt(c(sn, 16, 32), c("RU", 15, 256, 16), best, A.subtract)
 
     sent = [0]
 
-    def send(t):
+    def ways(t):
         dst = T.cores[target(rank, t, n)]
-        hs = helpers(core, dst, topo)
-        sn, ld = w("SN%d" % t), T["LD%d" % t]
+        return helpers(core, dst, topo) or [dst]
 
-        def emit():
-            order("G", [sn], [])
-            if not hs:
-                rid, pid = topo.addr(dst, core)
-                g.remote_dma(ld[:], sn[1], T.sem["arr%d" % t], T.sem.loc, pid, rid, topo.mask(core, dst))
-                sent[0] += len(topo.engines(core, dst))
-                return
-            tr = []
-            for i, (lo, hi) in enumerate(parts_of(len(hs))):
-                es = topo.engines(core, hs[i])
-                k = len(es) // len(hs)
-                rid, pid = topo.addr(hs[i], core)
-                tr.append(RemoteDMATransfer(dst_ids=[DstId(rid=rid, pnc=pid)], dma_engine_mask=emask(es[i * k:(i + 1) * k]),
-                                            remote_sem=T.sem["hop%d" % t], srcs=[T["SN%d" % t][:, lo:hi]], dsts=[ld[:, lo:hi]]))
-                sent[0] += k
-            g.remote_dma_fused(tr, local_sem=T.sem.loc)
-        return task("G", emit, [], [sn], 200, HOP * (2 if hs else 1))
+    def send(t):
+        def one(to, lo, hi):
+            def emit():
+                order("G", [c("SN%d" % t, lo, hi)], [])
+                rid, pid = topo.addr(to, core)
+                sem = T.sem[("arr0_%d" if to in T.cores else "hop%d") % t]
+                g.remote_dma(T["LD%d" % t][:, lo:hi], T["SN%d" % t][:, lo:hi], sem, T.sem.loc, pid, rid, topo.mask(core, to))
+                sent[0] += len(topo.engines(core, to))
+            x = task("G", emit, [], [c("SN%d" % t, lo, hi)], 200, (HOP if to in T.cores else HOPS) + (0 if t else FIRST))
+            x["first"] = 3
+            return x
+        return [one(to, lo, hi) for to, (lo, hi) in zip(ways(t), parts_of(len(ways(t))))]
 
     def kappa():
         ts(c("K1", 0, 1), c("UP", 257, 258), 32.0, A.mult)
@@ -672,67 +696,93 @@ def rank_program(g, core, T, topo):
         together([(c("VP", 0, 128), w("BH%d" % a1), c("RX", 128 * a1, 128 * a1 + 128), a1 == 0, a1 == 1) for a1 in (0, 1)])
         for par in (0, 1):
             ts(c("XP", 128 * par, 128 * par + 128), c("VP", 0, 128), later["won"][par], A.is_equal)
-        act(c("ZP", 0, 256), c("XP", 0, 256), F.Copy, scale=-2.0, bias=1.0)
         tt(c("XP", 512, 768), c("XP", 0, 256), w("DE"), A.mult)
-        tt(sg, c("ZP", 0, 256), sg, A.mult)
+        hold.append(tasks[-1])
+        act(c("ZP", 0, 256), c("XP", 0, 256), F.Copy, scale=-2.0, bias=1.0)
+        hold.pop()
         tt(e, c("XP", 512, 768), e, A.add)
+        tt(sg, c("ZP", 0, 256), sg, A.mult)
 
     def apply(t, own):
         src = T.cores[[r for r in range(n) if target(r, t, n) == rank][0]]
         hs = helpers(src, core, topo)
         ld = "LD%d" % t
-        count = sum(len(topo.engines(h, core)) for h in (hs or [src]))
-        task("R", lambda: note("R", "arr%d" % t, count, [], [w(ld)], {}), [w(ld)], [], 0, after=[own])
+
+        def lands(i, h, part):
+            task("R", lambda: note("R", "arr%d_%d" % (i, t), len(topo.engines(h, core)), [], [part], {}), [part], [], 0, after=[own[i]])
+        for i, (h, part) in enumerate(zip(hs or [src], parts_of(len(hs or [src])))):
+            lands(i, h, c(ld, *part))
         of = c("UP", 272, 288)
-        together([(of, w("I16"), c(ld, 256, 272), True, False), (of, w("IDN"), c(ld, 272, 288), False, True)], 2)
+        together([(of, w("I16"), c(ld, 0, 16), True, False), (of, w("IDN"), c(ld, 16, 32), False, True)], 2)
         ts(w("OU"), of, 4096.0, A.add)
-        tt(w("SH"), ind(w("XH"), w("OU")), c(ld, 0, 256), A.add)
+        tt(w("SH"), ind(w("XH"), w("OU")), c(ld, 32, SW), A.add)
         scatter(w("TB"), w("OU"), w("SH"))
 
+    first = len(tasks)
+    first_lists(0, ((0, HEAD // 128),))
     negate(0, 1024)
     negate(1024, 2048)
-    first_lists(0, ((0, HEAD // 128), (HEAD // 128, 4)))
+    for x in tasks[first:]:
+        x["first"] = 1
+    first_lists(0, ((HEAD // 128, 4),))
+    first = len(tasks)
     more_constants()
+    for x in tasks[first:]:
+        x["first"] = -1
     first_signs(0)
     shifted(c("EP", 0, 256), True)
+    for x in tasks[-2:]:
+        x["first"] = 3
     open_keys()
     for t in range(ROUNDS):
         cl, nx = t % 2, 1 - t % 2
         chains = {"e": hashes(cl, 0, 0, 2), "f": hashes(cl, 0, 2, 4), "g": hashes(cl, 1, 0, 2), "h": hashes(cl, 1, 2, 4)}
-        steps = {"z": gather_z, "r": relu, "s": restart, "b": balances, "q": odd_amounts, "y": far, "a": add_amounts,
-                 "o": lambda par, q: (over(par, q), count_over(par, q), sum_low(par, q)),
-                 "m": minus, "t": gate, "d": diff, "n": lambda q: sign("S", 0, q)}
-        fixed.extend("VS")
+        steps = {"z": gather_z, "r": relu, "s": restart, "b": balances, "q": odd_amounts, "u": sum_u, "o": over, "c": count_over,
+                 "w": sum_low, "y": far, "a": add_amounts, "k": minus, "m": plus, "j": sign_bank, "d": diff, "n": sign,
+                 "p": score, "t": gate, "x": add_gate, "i": sign_half, "v": low_abs, "l": low_bits}
+        fixed.extend("VSP")
         for step in ORDER.split():
             if step in chains:
                 chains[step].pop(0)()
             else:
                 steps[step[0]](*[int(x) if x.isdigit() else x for x in step[1:]])
+            if step[0] == "z":
+                tasks[-1]["first"] = 3
+            if step == "q3" and t == 0:
+                hold.append(tasks[-1])
+                kept = fixed[:]
+                del fixed[:]
+                group_constants()
+                for x in tasks[-4:]:
+                    x["first"] = -1
+                fixed.extend(kept)
+                hold.pop()
         del fixed[:]
         hold.append([x for x in tasks if x["q"] == "S"][-1])
-        moves()
-        if 0 < t < ROUNDS - 1:
-            next_lists(nx)
         for lo in range(0, EARLY, 256):
             halves(lo, lo + 256)
         hold.pop()
         if t == 0:
-            for lo in range(2048, TW, 384):
-                iota(c("XH", lo, lo + 384), [[0, 384]], 0, 0)
+            iota(c("XH", 4096, TW), [[0, TW - 4096]], 0, 0)
         first = len(tasks)
         fixed.append("V")
-        winners(t)
+        winners(t, parts_of(len(ways(t))))
         fixed.pop()
         for x in tasks[first:]:
             x["first"] = 3
-        hold.extend(tasks[-3:])
+        hold.extend(tasks[-2:])
         own = send(t)
         if t + 1 < ROUNDS:
             kappa()
-        for lo in range(EARLY, 2048, 256):
+        moves()
+        if 0 < t < ROUNDS - 1:
+            next_lists(nx)
+            tasks[-1]["first"] = -1
+        for lo in range(EARLY, 2048 if t else 4096, 256):
             halves(lo, lo + 256)
             tasks[-1]["first"] = -1
         if t == 0:
+            spread_constants()
             first_lines(0)
             first_lists(1, ((0, 4),))
             first_signs(1)
@@ -746,11 +796,14 @@ def rank_program(g, core, T, topo):
             negate(0, 2048)
         for x in tasks[first:]:
             x["first"] = 3
+        first = len(tasks)
         flips(cl)
         if t == 0:
             back_constants()
         if t + 2 >= ROUNDS:
             outputs(cl)
+        for x in tasks[first + LATE:]:
+            x["first"] = -1
         if t + 1 < ROUNDS:
             open_keys()
         del hold[:]

import numpy as np
from concourse.bass import DstId, RemoteDMATransfer
from concourse.mybir import dt, AluOpType, AxisListType, ActivationFunctionType

ROUNDS = 4
SW = 288
TW = 4352
NEG = 1408
EARLY = 1024
HEAD = 256
LATE = 6
HOPS, FIRST = 3000, 2000
XT = 500
TOP = 16777215
FLOOR = -16384
ORDER = """
zS001 zV101 zS012 zS112 zS024 zS124 w00 u002
r10 r00 o00 c00 w01 s0 r01 b0 e r11 e q0 k0 e b1 e o01 e u024 w02 w03 c01 q1 e f e y002 a02 u102 w10 w11 k1
f o02 f o03 f r02 f g s2 f g f y024 a24 r03 g r12 g o10 g r13 g o11 g c02 c03 c10 c11 y101 y112
b2 b3 m0 q2 w12 q3 u124 o12 o13 nV00 h h h h h h h j0 nS01 m1 c12 c13 w13 j1 nS02 nS03 t v
p10 p00 p01 p11 p02 p03 x d2 iS20 d3 iV21 p12 nV13 p13 l0 l1
"""
WAKE, GATHER, SCATTER, MATMUL, LOAD, HOP, ADD, SLACK, EAGER = 100, 1.25, 3.5, 0.6, 1800, 2000, 3000, 200, 30
SCRATCH = {
    "TB": ("sbuf", [128, TW], "bfloat16"), "XH": ("sbuf", [128, TW], "float32"),
    "LEDI": ("sbuf", [128, 512], "int32"), "MKI": ("sbuf", [128, 512], "bfloat16"), "EF": ("sbuf", [128, 256], "float32"),
    "YLB": ("sbuf", [128, 512], "float32"), "YMB": ("sbuf", [128, 512], "bfloat16"),
    "ZQ": ("sbuf", [128, 10240], "bfloat16"),
    "MX": ("sbuf", [128, 4096], "bfloat16"), "SB": ("sbuf", [128, 4096], "bfloat16"), "DC": ("sbuf", [128, 2048], "bfloat16"),
    "D": ("sbuf", [128, 4096], "bfloat16"), "ZB": ("sbuf", [128, 4096], "bfloat16"), "DS": ("sbuf", [128, 4096], "bfloat16"),
    "UI": ("sbuf", [128, 256], "int32"), "UM": ("sbuf", [128, 256], "int32"), "PF": ("sbuf", [128, 256], "float32"),
    "HI": ("sbuf", [128, 256], "int32"), "HH": ("sbuf", [128, 256], "int32"), "HS": ("sbuf", [128, 256], "float32"),
    "HO": ("sbuf", [128, 256], "uint16"), "OFF": ("sbuf", [128, 256], "uint16"),
    "IDF": ("sbuf", [128, 128], "float32"), "NDF": ("sbuf", [128, 128], "float32"),
    "KA": ("sbuf", [128, 256], "float32"), "GG": ("sbuf", [128, 256], "bfloat16"), "RM": ("sbuf", [128, 256], "float32"),
    "KU": ("sbuf", [128, 256], "float32"), "RU": ("sbuf", [128, 256], "float32"),
    "MI": ("sbuf", [128, 16], "int32"), "EB": ("sbuf", [128, 16], "int32"), "KI": ("sbuf", [128, 256], "int32"),
    "FL": ("sbuf", [128, 16], "bfloat16"), "CU": ("sbuf", [128, 16], "bfloat16"),
    "C255": ("sbuf", [128, 16], "bfloat16"), "N512": ("sbuf", [128, 128], "bfloat16"), "IX": ("sbuf", [128, 16], "int32"),
    "IXU": ("sbuf", [128, 16], "uint16"), "KL": ("sbuf", [128, 256], "int32"), "OU": ("sbuf", [128, 16], "uint16"),
    "KV": ("sbuf", [128, 16], "bfloat16"), "RX": ("sbuf", [128, 256], "bfloat16"),
    "SH": ("sbuf", [128, 256], "int32"), "DE": ("sbuf", [128, 256], "float32"),
    "K1": ("sbuf", [128, 8], "int32"), "K2": ("sbuf", [128, 8], "int32"), "K3": ("sbuf", [128, 8], "float32"),
    "PI": ("sbuf", [128, 8], "int32"), "PB": ("sbuf", [128, 8], "int32"), "PN": ("sbuf", [128, 8], "float32"),
    "PD": ("sbuf", [128, 24], "float32"),
    "IM": ("sbuf", [128, 144], "float32"), "IG": ("sbuf", [128, 128], "float32"), "I2": ("sbuf", [128, 16], "float32"),
    "FA": ("sbuf", [128, 136], "float32"), "BA": ("sbuf", [128, 136], "float32"),
    "BD": ("sbuf", [128, 128], "bfloat16"), "IDN": ("sbuf", [128, 128], "bfloat16"), "NID": ("sbuf", [128, 128], "bfloat16"),
    "I16": ("sbuf", [128, 128], "bfloat16"), "ONE": ("sbuf", [128, 128], "bfloat16"),
    "C2": ("sbuf", [128, 128], "bfloat16"), "LT": ("sbuf", [128, 128], "bfloat16"),
    "CW": ("sbuf", [128, 144], "bfloat16"), "UW": ("sbuf", [128, 144], "bfloat16"), "VW": ("sbuf", [128, 144], "bfloat16"),
    "KC": ("sbuf", [128, 256], "bfloat16"), "KX": ("sbuf", [128, 256], "bfloat16"), "KR": ("sbuf", [128, 256], "bfloat16"),
    "KD": ("sbuf", [128, 256], "float32"), "KE": ("sbuf", [128, 256], "float32"),
    "I8K": ("sbuf", [128, 128], "bfloat16"), "IR": ("sbuf", [128, 128], "bfloat16"),
    "RI": ("sbuf", [128, 256], "bfloat16"), "RK": ("sbuf", [128, 256], "bfloat16"), "CL": ("sbuf", [128, 16], "uint16"),
    "ZZ": ("sbuf", [128, 16], "bfloat16"),
    "XP": ("psum", [128, 1024], "float32"), "KP": ("psum", [128, 512], "float32"), "UP": ("psum", [128, 512], "float32"),
    "VP": ("psum", [128, 512], "float32"), "ZP": ("psum", [128, 512], "float32"), "EP": ("psum", [128, 512], "float32"),
    "FP": ("psum", [128, 512], "float32"),
}
for _c in range(2):
    SCRATCH["E%d" % _c] = ("sbuf", [128, 256], "float32")
    SCRATCH["SG%d" % _c] = ("sbuf", [128, 256], "float32")
    SCRATCH["FA%d" % _c] = ("sbuf", [128, 136], "float32")
    SCRATCH["FB%d" % _c] = ("sbuf", [128, 136], "bfloat16")
    SCRATCH["BA%d" % _c] = ("sbuf", [128, 136], "float32")
    SCRATCH["BB%d" % _c] = ("sbuf", [128, 136], "bfloat16")
    SCRATCH["BH%d" % _c] = ("sbuf", [128, 128], "bfloat16")
    SCRATCH["TS%d" % _c] = ("sbuf", [128, 144], "bfloat16")
for _t in range(ROUNDS):
    SCRATCH["SN%d" % _t] = ("sbuf", [128, SW], "bfloat16")
    SCRATCH["LD%d" % _t] = ("sbuf", [128, SW], "bfloat16")
SEMAPHORES = (["qV", "qS", "qP", "qG", "loc"] + ["d%d" % i for i in range(10)] + ["a%d" % i for i in range(4)]
              + ["%s%d" % (s, t) for s in ("arr0_", "arr1_", "hop") for t in range(ROUNDS)])


def helpers(core, dst, topo):
    if topo.may_write(core, dst):
        return []
    own = [c for c in topo.cores_of(core) if c != core and topo.may_write(c, dst)]
    near = [c for c in own if topo.die(c) == topo.die(core)]
    return (near or own)[:2]


def target(rank, t, n):
    return (rank + 1 + t % (n - 1)) % n


def parts_of(n):
    cuts = [0] + [SW * i // n // 32 * 32 + 32 for i in range(1, n)] + [SW]
    return list(zip(cuts, cuts[1:]))


def bridge(g, core, T, topo):
    n = len(T.cores)
    sent = 0
    for t in range(ROUNDS):
        for r in range(n):
            src, dst = T.cores[r], T.cores[target(r, t, n)]
            hs = helpers(src, dst, topo)
            if core not in hs:
                continue
            lo, hi = parts_of(len(hs))[hs.index(core)]
            g.wait_ge(T.sem["hop%d" % t], len(topo.engines(src, core)))
            rid, pid = topo.addr(dst, core)
            piece = T["LD%d" % t][:, lo:hi]
            g.remote_dma(piece, piece, T.sem["arr%d_%d" % (hs.index(core), t)], T.sem.loc, pid, rid, topo.mask(core, dst))
            sent += len(topo.engines(core, dst))
    if sent:
        g.wait_ge(T.sem.loc, sent)


def rank_program(g, core, T, topo):
    rank = T.rank_of(core)
    if rank is None:
        bridge(g, core, T, topo)
        return
    A, F = AluOpType, ActivationFunctionType
    n = len(T.cores)
    Qs = {"V": g.vector, "S": g.scalar, "P": g.tensor, "G": g, "Y": g.sync}
    seq = {"V": 0, "S": 0, "P": 0, "G": 0}
    known = {q: {} for q in Qs}
    log = {}
    masks = {}

    def c(name, lo, hi, step=1):
        key = (name, lo, hi, step)
        if key not in masks:
            bits = np.zeros(SCRATCH[name][1][1], np.uint8)
            bits[lo:hi:step] = 1
            exact = int.from_bytes(np.packbits(bits).tobytes(), "big")
            bank = exact
            if SCRATCH[name][0] == "psum":
                wide = bits.copy()
                for b in range(0, bits.size, 512):
                    if bits[b:b + 512].any():
                        wide[b:b + 512] = 1
                bank = int.from_bytes(np.packbits(wide).tobytes(), "big")
            masks[key] = (exact, bank)
        ap = T[name][:, lo:hi:step] if step != 1 else T[name][:, lo:hi]
        return (name, ap, masks[key][0], masks[key][1], len(range(lo, hi, step)))

    def w(name):
        return c(name, 0, SCRATCH[name][1][1])

    def order(q, reads, writes):
        need = {}
        for isw, lst in ((False, reads), (True, writes)):
            for name, _, ex, bk, _n in lst:
                psum = SCRATCH[name][0] == "psum"
                for rq, src, cnt, rw, rex, rbk, clk in log.get(name, []):
                    if psum and rq != q:
                        hit = bk & rbk
                    elif psum and q == "P":
                        hit = 0
                    else:
                        hit = (isw or rw) and (ex & rex)
                    if hit and need.get(src, (0, None))[0] < cnt:
                        need[src] = (cnt, clk)
        for src in sorted(need, key=lambda s: -len(need[s][1])):
            cnt, clk = need[src]
            if known[q].get(src, 0) < cnt:
                Qs[q].wait_ge(T.sem[src], cnt)
                for s, v in clk.items():
                    known[q][s] = max(known[q].get(s, 0), v)
                known[q][src] = max(known[q].get(src, 0), cnt)

    def note(q, src, cnt, reads, writes, clk):
        for isw, lst in ((False, reads), (True, writes)):
            for name, _, ex, bk, _n in lst:
                old = log.get(name, [])
                if isw:
                    old = [x for x in old if x[4] & ~ex]
                old.append((q, src, cnt, isw, ex, bk, clk))
                log[name] = old

    tasks, group, hold = [], [], []

    fixed = []

    def task(q, emit, writes, reads, cost, lag=0, adds=False, after=()):
        if group:
            x = group[0]
            x["emit"].append(emit)
            x["writes"] += writes
            x["reads"] += reads
            x["cost"] += cost
            x["adds"] = adds
            return x
        tasks.append({"q": q, "emit": [emit], "writes": list(writes), "reads": list(reads), "cost": cost, "lag": lag,
                      "adds": adds, "after": list(after) + hold, "fixed": q in fixed, "first": 0})
        return tasks[-1]

    def together(calls, first=0):
        x = {"q": "P", "emit": [], "writes": [], "reads": [], "cost": 0, "lag": 0, "adds": False, "after": list(hold),
             "fixed": "P" in fixed, "first": first}
        tasks.append(x)
        group.append(x)
        for args in calls:
            mm(*args)
        group.pop()

    def run(q, fn, writes, reads, cost, adds=False):
        def emit():
            order(q, reads, writes)
            src = "q" + q
            fn(Qs[q]).then_inc(T.sem[src], 1)
            seq[q] += 1
            clk = dict(known[q])
            clk[src] = seq[q]
            note(q, src, seq[q], reads, writes, clk)
        task(q, emit, writes, reads, cost, 0, adds)

    moved = {}

    def dma(q, sem, out, in_, lag, add=False):
        writes = [out] if isinstance(out, tuple) else []
        reads = ([in_] if isinstance(in_, tuple) else []) + (writes if add else [])

        def emit():
            order(q, reads, writes)
            kw = {"accum_op": A.add} if add else {}
            Qs[q].dma_start(out[1] if writes else out, in_[1] if reads else in_, **kw).then_inc(T.sem[sem], 16)
            moved[sem] = moved.get(sem, 0) + 16
            note(q, sem, moved[sem], reads, writes, dict(known[q]))
        task(q, emit, writes, reads, 300 if add else 64, lag)

    def links():
        seen, last = {}, {}
        for i, x in enumerate(tasks):
            x["i"] = i
            pre = set(y["i"] for y in x["after"])
            for isw, lst in ((False, x["reads"]), (True, x["writes"])):
                for a in lst:
                    for j, wrote, ex, bk in seen.get(a[0], []):
                        if isw and wrote and x["q"] == tasks[j]["q"] == "P":
                            if bk & a[3] and not (x["adds"] and tasks[j]["adds"]):
                                pre.add(j)
                        elif (isw or wrote) and ex & a[2]:
                            pre.add(j)
            for isw, lst in ((False, x["reads"]), (True, x["writes"])):
                for a in lst:
                    old = seen.get(a[0], [])
                    if isw and not x["adds"]:
                        old = [y for y in old if y[2] & ~a[2]]
                    seen[a[0]] = old + [(i, isw, a[2], a[3])]
            pre.discard(i)
            x["behind"] = None
            if x["fixed"]:
                if x["q"] in last and last[x["q"]] not in pre:
                    x["behind"] = last[x["q"]]
                    pre.add(x["behind"])
                last[x["q"]] = i
            x["pre"], x["post"] = pre, set()
            for j in pre:
                tasks[j]["post"].add(i)
            x["banks"] = set((a[0], a[3]) for a in x["reads"] + x["writes"] if SCRATCH[a[0]][0] == "psum")

    def issue():
        links()
        left = [len(x["pre"]) for x in tasks]
        free, used, base = {}, {}, [0] * len(tasks)
        ready = [x for x in tasks if not x["pre"]]
        while ready:
            at = {}
            for x in ready:
                t = max(free.get(x["q"], 0), base[x["i"]])
                for name, bk in x["banks"]:
                    for q, b, e in used.get(name, []):
                        if q != x["q"] and b & bk:
                            t = max(t, e + WAKE)
                at[x["i"]] = t
            q = min(ready, key=lambda y: (at[y["i"]], y["i"]))["q"]
            mine = sorted([y for y in ready if y["q"] == q], key=lambda y: (-y["first"], y["i"]))
            x = mine[0]
            for y in mine[1:]:
                if at[y["i"]] + EAGER < at[x["i"]] and at[y["i"]] + y["cost"] <= at[mine[0]["i"]] + (0 if mine[0]["first"] == 3 else SLACK):
                    x = y
            ready.remove(x)
            free[q] = at[x["i"]] + x["cost"]
            for name, bk in x["banks"]:
                used[name] = [u for u in used.get(name, []) if not (u[0] == q and u[1] == bk)] + [(q, bk, free[q])]
            for f in x["emit"]:
                f()
            for j in x["post"]:
                base[j] = max(base[j], free[q] + x["lag"] + (0 if q == tasks[j]["q"] == "P" or tasks[j]["behind"] == x["i"] else WAKE))
                left[j] -= 1
                if not left[j]:
                    ready.append(tasks[j])

    def ind(win, off):
        return ("ind", win, off)

    def opnd(x, reads):
        if x[0] == "ind":
            reads += [x[1], x[2]]
            return x[1][1].indirect(x[2][1])
        reads.append(x)
        return x[1]

    def sc(x, reads):
        return opnd(x, reads) if isinstance(x, tuple) else x

    def cycles(out, ins, rate=None):
        if ins and ins[0][0] == "ind":
            return 70 + GATHER * out[4]
        if rate is None:
            rate = 0.5 if all(SCRATCH[x[0]][2] in ("bfloat16", "uint16") for x in [out] + ins) else 1
        return max(64, rate * out[4])

    def tt(out, in0, in1, op):
        r = []
        i0, i1 = opnd(in0, r), opnd(in1, r)
        rate = 1 if "psum" in [SCRATCH[x[0]][0] for x in r] else 2
        run("V", lambda e: e.tensor_tensor(out[1], i0, i1, op), [out], r, cycles(out, [in0, in1], rate))

    def ts(out, in0, s1, op0, s2=None, op1=None):
        r = []
        i0, x1 = opnd(in0, r), sc(s1, r)
        if op1 is None:
            run("V", lambda e: e.tensor_scalar(out[1], i0, x1, None, op0), [out], r, cycles(out, [in0]))
        else:
            x2 = sc(s2, r)
            run("V", lambda e: e.tensor_scalar(out[1], i0, x1, x2, op0, op1), [out], r, cycles(out, [in0]))

    def cp(out, in_):
        r = []
        i0 = opnd(in_, r)
        run("V", lambda e: e.tensor_copy(out[1], i0), [out], r, cycles(out, [in_]))

    def scatter(win, off, in_):
        run("V", lambda e: e.tensor_copy(win[1].indirect(off[1]), in_[1]), [win], [in_, off], 60 + SCATTER * in_[4])

    def scan(out, d0, d1, op0, op1, initial=0.0):
        run("V", lambda e: e.tensor_tensor_scan(out[1], d0[1], d1[1], initial, op0, op1), [out], [d0, d1], cycles(out, [d0, d1]))

    def fill(out, v):
        run("V", lambda e: e.memset(out[1], v), [out], [], cycles(out, []))

    def act(out, in_, func, scale=None, bias=None):
        r = []
        i0 = opnd(in_, r)
        kw = {}
        if scale is not None:
            kw["scale"] = sc(scale, r)
        if bias is not None:
            kw["bias"] = sc(bias, r)
        run("S", lambda e: e.activation(out[1], i0, func, **kw), [out], r, cycles(out, [in_], 1))

    def mm(out, lhsT, rhs, start=True, stop=True, adds=False):
        cost = MATMUL * max(64, out[4]) * (4 if SCRATCH[rhs[0]][2] == "float32" else 1)
        run("P", lambda e: e.matmul(out[1], lhsT[1], rhs[1], start, stop), [out], [lhsT, rhs], cost, adds)

    def iota(out, pattern, base, cm, flag=True):
        if flag:
            run("G", lambda e: e.iota(out[1], pattern, base, cm, allow_small_or_imprecise_dtypes=True), [out], [], 160 + 2 * out[4])
        else:
            run("G", lambda e: e.iota(out[1], pattern, base, cm), [out], [], 160 + 2 * out[4])

    dma("Y", "d0", c("LEDI", 0, HEAD), T.led[:, 0:HEAD], LOAD)
    dma("S", "d1", c("MKI", 0, HEAD), T.mk[:, 0:HEAD], LOAD)
    dma("Y", "d2", c("TB", 0, 1024), T.xt[:, 0:1024], LOAD + XT)
    dma("S", "d6", c("TB", 1024, 2048), T.xt[:, 1024:2048], LOAD + 2 * XT)
    dma("Y", "d7", c("LEDI", HEAD, 512), T.led[:, HEAD:512], LOAD + 3 * XT)
    dma("S", "d8", c("MKI", HEAD, 512), T.mk[:, HEAD:512], LOAD + 3 * XT)

    iota(c("PI", 0, 1), [[0, 1]], 0, 1, False)
    iota(w("IM"), [[1, 144]], 0, 0)
    iota(c("DC", 0, 1024), [[0, 512], [-4096, 2]], 4096, 0)
    dma("Y", "d9", c("DC", 1024, 2048), c("DC", 0, 1024), LOAD)
    for q in range(4):
        iota(c("ZQ", 4096 + 1024 * q, 5120 + 1024 * q, 2), [[0, 512]], -4096, 0)
    iota(w("KC"), [[0, 16], [-16, 8], [-9, 2]], -7, 0)
    iota(c("KX", 0, 256, 2), [[1, 128]], 0, 0)
    iota(c("KX", 1, 256, 2), [[2, 128]], 1, 0)
    iota(w("KR"), [[0, 128], [128, 2]], 128, 0)
    iota(w("IG"), [[1, 16], [0, 8]], 0, 0)
    iota(w("I2"), [[1, 2], [0, 8]], 0, 0)
    iota(w("RI"), [[0, 2], [1, 16], [0, 8]], 0, 0)
    for name, pattern, floor in (("KD", [[0, 16]], FLOOR), ("KE", [[-1, 16]], FLOOR + 15)):
        iota(w(name), [[0, 256]], TOP, 0)
        iota(c(name, 0, 256, 16), pattern, floor, 0)

    fields = ((0, 127), (4, 7), (0, 15), (0, 1), (1, 7), (0, 7), (3, 1))
    for i, (sh, mk) in enumerate(fields):
        ts(c("PB", i, i + 1), c("PI", 0, 1), sh, A.arith_shift_right, mk, A.bitwise_and)
    cp(c("PN", 0, 7), c("PB", 0, 7))
    pp, pg, pr, podd, phalf, p7, phigh = [c("PN", i, i + 1) for i in range(7)]
    col = [0]

    def column(src, s1, op0, s2, op1):
        out = c("PD", col[0], col[0] + 1)
        col[0] += 1
        ts(out, src, s1, op0, s2, op1)
        return out

    g16 = column(pg, 16.0, A.mult, 15.0, A.add)
    peven = column(podd, -1.0, A.mult, 1.0, A.add)
    fwd = column(phalf, g16, A.add, -7.0, A.add)
    par_of = (peven, podd)
    mneg = [column(x, -2048.0, A.mult, 0.0, A.add) for x in par_of]
    ts(w("FA"), c("IM", 0, 136), fwd, A.is_equal)
    for i in (0, 1):
        act(w("FA%d" % i), w("FA"), F.Copy, scale=par_of[i])
        act(w("FB%d" % i), w("FA"), F.Copy, scale=mneg[i])
    pw = column(pr, 2.0, A.mult, 1.0, A.add)
    p27 = column(p7, 2.0, A.mult, 0.0, A.add)
    pv = column(p7, 2.0, A.mult, 1.0, A.add)
    ts(w("CW"), w("IM"), g16, A.is_equal)
    ts(w("IDN"), c("IM", 0, 128), pp, A.is_equal)
    fill(w("C2"), 2048.0)
    act(w("UW"), w("CW"), F.Copy, scale=pw)
    act(w("VW"), w("CW"), F.Copy, scale=pv)

    later = {}

    def more_constants():
        won = [column(p27, -1.0, A.mult, 15.0 - i, A.add) for i in (0, 1)]
        half = [column(pg, 2.0, A.mult, float(i), A.add) for i in (0, 1)]
        bwd = column(p27, g16, A.add, -14.0, A.add)
        plow = column(phigh, -1.0, A.mult, 1.0, A.add)
        later.update(won=won, bwd=bwd, high=(plow, phigh))
        later.update(half=half)
        ts(w("NID"), w("IDN"), -1.0, A.mult)
        ts(w("I8K"), w("IDN"), 8192.0, A.mult)
        ts(w("IR"), w("IDN"), pr, A.mult)
        ts(w("TS0"), w("CW"), 1048576.0, A.mult)
        ts(w("TS1"), w("CW"), -1048576.0, A.mult)
        ts(w("N512"), w("IDN"), -512.0, A.mult)
        ts(w("I16"), w("IDN"), 16.0, A.mult)
        fill(w("ONE"), 1.0)
        fill(w("ZZ"), 0.0)
        fill(w("C255"), 255.0)

    def group_constants():
        for i in (0, 1):
            ts(w("BH%d" % i), w("IG"), later["half"][i], A.is_equal)
        tt(w("BD"), w("BH0"), w("BH1"), A.add)
        run("G", lambda e: e.affine_select(w("LT")[1], w("BD")[1], [[1, 128]], A.is_gt, 0.0, 0, -1), [w("LT")], [w("BD")], 460)

    def spread_constants():
        ts(w("CL"), w("I2"), p27, A.add)
        ts(w("RK"), w("RI"), pr, A.is_equal)

    def back_constants():
        act(w("IDF"), w("IDN"), F.Copy)
        act(w("NDF"), w("IDN"), F.Copy, scale=-1024.0)
        ts(w("BA"), c("IM", 0, 136), later["bwd"], A.is_equal)
        for i in (0, 1):
            act(w("BA%d" % i), w("BA"), F.Copy, scale=later["high"][i])
            act(w("BB%d" % i), w("BA"), F.Copy, scale=later["high"][i])

    def to_lists(cl, outs, lo, hi, lines, marks, base=False):
        for par, (name, at) in enumerate(outs):
            o = c(name, at + 32 * lo, at + 32 * hi)
            steps = [(w("IDN"), c("C2", 0, o[4]))] if base else []
            for a1 in (0, 1):
                if lines:
                    steps.append((c("FA%d" % par, 8 - 8 * a1, 136 - 8 * a1), c("EF", 64 * lo + a1, 64 * hi, 2)))
                if marks:
                    steps.append((c("FB%d" % par, 8 - 8 * a1, 136 - 8 * a1), c("MKI", 128 * lo + cl + 2 * a1, 128 * hi, 4)))
            together([(o, l, r, i == 0, i == len(steps) - 1) for i, (l, r) in enumerate(steps)])

    def to_rows(out, src, by):
        for a1 in (0, 1):
            together([(c(out, a1, 256, 2), c(by % a1, 1 - par, 129 - par), c(src, 128 * par, 128 * par + 128), par == 0, par == 1)
                      for par in (0, 1)])

    def first_lists(cl, parts):
        outs = (("KP", 0), ("FP", 0))
        for lo, hi in parts:
            cp(c("EF", 64 * lo, 64 * hi), c("LEDI", 128 * lo + cl, 128 * hi, 2))
            to_lists(cl, outs, lo, hi, True, True)
            for par, (name, at) in enumerate(outs):
                ts(lists("OFF", par, lo, hi), c(name, at + 32 * lo, at + 32 * hi), 2048.0, A.add)
            to_lists(cl, (("EP", 256), ("EP", 384)), lo, hi, False, True, True)
            to_lists(cl, (("EP", 0), ("EP", 128)), lo, hi, True, False)

    def first_signs(cl):
        act(w("SG%d" % cl), c("EP", 256, 512), F.Copy, scale=-1.0 / 1024.0, bias=1.0)

    def first_lines(cl):
        act(w("E%d" % cl), c("EP", 0, 256), F.Copy)

    def next_lists(cl):
        act(c("EP", 256, 512), w("SG%d" % cl), F.Copy, scale=-1024.0, bias=1024.0)
        act(c("EP", 0, 256), w("E%d" % cl), F.Copy)
        o = c("FP", 256, 512)
        together([(o, w("IDF"), w("E%d" % cl), True, False), (o, w("NDF"), w("SG%d" % cl), False, True)])
        ts(w("OFF"), o, 1024.0, A.add)

    def shifted(src, first):
        if first:
            act(c("FP", 0, 256), src, F.Copy, scale=32.0)
        else:
            act(c("FP", 0, 256), src, F.Identity, scale=32.0, bias=c("K3", 0, 1))

    def outputs(cl):
        to_rows("VP", "E%d" % cl, "BA%d")
        act(w("GG"), w("SG%d" % cl), F.Copy, scale=0.5, bias=0.5)
        to_rows("ZP", "GG", "BB%d")
        act(c("YLB", cl, 512, 2), c("VP", 0, 256), F.Copy)
        act(c("YMB", cl, 512, 2), c("ZP", 0, 256), F.Copy)

    Z, ZE = 4096, 8192

    def table():
        return c("TB", 0, 4096)

    def lists(name, par, lo, hi):
        return c(name, 128 * par + 32 * lo, 128 * par + 32 * hi)

    def packed(name, par, lo, hi):
        return c(name, 2048 * par + 512 * lo, 2048 * par + 512 * hi)

    def amounts(par, lo, hi):
        return c("ZQ", 1024 * lo + 1, 1024 * hi, 2) if par else c("ZQ", ZE + 512 * lo, ZE + 512 * hi)

    def items(par, lo, hi):
        return c("ZQ", Z + 1024 * lo + 1, Z + 1024 * hi, 2) if par else amounts(0, lo, hi)

    def gather_z(eng, par, lo, hi):
        out, src = items(par, lo, hi), ind(table(), lists("OFF", par, lo, hi))
        if eng == "S":
            act(out, src, F.Copy)
        else:
            cp(out, src)

    def relu(par, q):
        ts(c("MX", 1024 * q + par, 1024 * q + 1024, 2), items(par, q, q + 1), 0.0, A.max)

    def restart(q):
        ts(c("DC", 0, 2048, 16), c("ZQ", ZE + 512 * q, ZE + 512 * q + 1024, 8), 0.0, A.max)

    def balances(q):
        scan(c("SB", 1024 * q, 1024 * q + 1024), c("MX", 1024 * q, 1024 * q + 1024),
             c("DC", 1024 * (q % 2), 1024 * (q % 2) + 1024), A.subtract, A.min)

    def odd_amounts(q):
        lo, hi = 1024 * q, 1024 * q + 1024
        scan(c("ZQ", lo, hi), c("ZQ", Z + lo, Z + hi), c("SB", lo, hi), A.min, A.max)

    def sum_u(par, lo, hi):
        def cols(row):
            if par:
                return c("ZQ", 1024 * lo + 2 * row + 1, 1024 * hi, 32)
            return c("ZQ", ZE + 512 * lo + row, ZE + 512 * hi, 16)
        together([(lists("UP", par, lo, hi), c("UW", 15 - row, 143 - row), cols(row), row == 0, row == 15) for row in range(16)], 2)

    def hashes(cl, par, lo, hi):
        s = (128 * par + 32 * lo, 128 * par + 32 * hi)
        nm = c("EP", 256 + s[0], 256 + s[1])
        return [lambda: tt(c("UI", *s), c("UP", *s), c("SG%d" % cl, *s), A.mult),
                lambda: ts(c("UM", *s), c("UI", *s), 2047, A.bitwise_and),
                lambda: tt(c("PF", *s), c("UM", *s), c("EP", *s), A.mult),
                lambda: tt(c("HI", *s), c("PF", *s), c("FP", *s), A.add),
                lambda: ts(c("HH", *s), c("HI", *s), 5, A.arith_shift_right, 2047, A.bitwise_and),
                lambda: tt(c("HS", *s), c("HH", *s), nm, A.add if par else A.subtract),
                lambda: ts(c("HO", *s), c("HS", *s), 0.0 if par else 2048.0, A.add)]

    def sum_low(par, q):
        def cols(row):
            if par:
                return c("ZQ", 256 * row + 1, 256 * row + 256, 2)
            return c("ZQ", ZE + 128 * row, ZE + 128 * row + 128)
        together([(c("VP", par, 256, 2), c("VW", 15 - row, 143 - row), cols(row), row == 0, row == 15)
                  for row in range(4 * q, 4 * q + 4)], par)

    def over(par, q):
        ts(packed("ZB", par, q, q + 1), amounts(par, q, q + 1), 0.0, A.not_equal)

    def count_over(par, q):
        at = 2048 * par
        together([(c("ZP", par, 256, 2), c("CW", 15 - row, 143 - row), c("ZB", at + 128 * row, at + 128 * row + 128),
                   row == 0, row == 15) for row in range(4 * q, 4 * q + 4)], par)

    def open_keys():
        together([(c("KP", 0, 256), w(l), w(r), l == "I8K", False) for l, r in (("I8K", "KC"), ("IDN", "KX"), ("IR", "KR"))])

    def score(par, q):
        at, last = 2048 * par, (par, q) == (1, 3)
        together([(c("KP", par, 256, 2), c("TS%d" % par, 15 - row, 143 - row), c("DS", at + 128 * row, at + 128 * row + 128),
                   False, last and row == 15, not last) for row in range(4 * q, 4 * q + 4)])

    def gate():
        act(w("GG"), c("ZP", 0, 256), F.Relu, scale=-33554432.0, bias=9 * 33554432.0)

    def add_gate():
        mm(c("KP", 0, 256), w("NID"), w("GG"), False, False, True)

    def far(par, lo, hi):
        act(packed("D", par, lo, hi), ind(table(), lists("HO", par, lo, hi)), F.Copy)

    def add_amounts(lo, hi):
        dma("G", "a%d" % lo, packed("D", 0, lo, hi), amounts(0, lo, hi), ADD, True)
        tasks[-1]["first"] = 3

    def bank(q):
        return c("XP", 512 * q, 512 * q + 512)

    def minus(q):
        mm(bank(q), w("NID"), amounts(1, q, q + 1), True, False)

    def plus(q):
        mm(bank(q), w("IDN"), packed("D", 1, q, q + 1), False, True)

    def sign_bank(q):
        act(packed("DS", 1, q, q + 1), bank(q), F.Sign)

    def sign(eng, par, q):
        if eng == "S":
            act(packed("DS", par, q, q + 1), packed("D", par, q, q + 1), F.Sign)
        else:
            ts(packed("DS", par, q, q + 1), packed("D", par, q, q + 1), 1.0, A.min, -1.0, A.max)

    def sign_half(eng, q, h):
        lo = 2048 + 512 * q + 256 * h
        if eng == "S":
            act(c("DS", lo, lo + 256), c("D", lo, lo + 256), F.Sign)
        else:
            ts(c("DS", lo, lo + 256), c("D", lo, lo + 256), 1.0, A.min, -1.0, A.max)

    def diff(q):
        tt(packed("D", 1, q, q + 1), ind(table(), lists("HO", 1, q, q + 1)), amounts(1, q, q + 1), A.subtract)

    def halves(lo, hi):
        act(c("XH", lo, hi), c("TB", lo, hi), F.Copy, scale=0.5, bias=-0.25)

    def negate(lo, hi):
        cut = lo + (hi - lo) * NEG // 2048
        ts(c("TB", 2048 + lo, 2048 + cut), c("TB", lo, cut), -1.0, A.mult)
        act(c("TB", 2048 + cut, 2048 + hi), c("TB", cut, hi), F.Copy, scale=-1.0)

    def low_abs():
        act(w("KA"), c("VP", 0, 256), F.Abs)

    def low_bits(i):
        if i:
            ts(w("KL"), w("KI"), 15, A.bitwise_and)
        else:
            cp(w("KI"), w("KA"))

    def winners(t, parts):
        sn = "SN%d" % t
        best = c("RM", 15, 256, 16)
        scan(w("RM"), w("KD"), c("KP", 0, 256), A.min, A.max, float(TOP))
        tt(w("KU"), c("KP", 0, 256), w("KL"), A.add)
        cp(w("MI"), best)
        ts(w("FL"), best, -0.5, A.is_ge)
        ts(w("IX"), w("MI"), 16383, A.bitwise_and)
        scan(w("CU"), w("FL"), w("ZZ"), A.add, A.max)
        cp(w("IXU"), w("IX"))
        for lo, hi in parts:
            lo = max(lo, 32)
            act(c(sn, lo, hi), ind(w("ZQ"), c("IXU", lo // 16 - 2, hi // 16 - 2)), F.Abs, scale=0.5)
        scan(w("RU"), w("KE"), w("KU"), A.min, A.max, float(TOP))
        pl = c("UP", 288, 304)
        together([(c("UP", 256, 257), w("LT"), c("CU", 15, 16)), (pl, w("IDN"), w("CU"), True, False),
                  (pl, w("N512"), w("FL"), False, False), (pl, w("IDN"), w("C255"), False, True),
                  (c("UP", 257, 258), w("ONE"), c("CU", 15, 16))])
        ts(c(sn, 0, 16), pl, c("UP", 256, 257), A.add, pr, A.min)
        tt(c(sn, 16, 32), c("RU", 15, 256, 16), best, A.subtract)

    sent = [0]

    def ways(t):
        dst = T.cores[target(rank, t, n)]
        return helpers(core, dst, topo) or [dst]

    def send(t):
        def one(to, lo, hi):
            def emit():
                order("G", [c("SN%d" % t, lo, hi)], [])
                rid, pid = topo.addr(to, core)
                sem = T.sem[("arr0_%d" if to in T.cores else "hop%d") % t]
                g.remote_dma(T["LD%d" % t][:, lo:hi], T["SN%d" % t][:, lo:hi], sem, T.sem.loc, pid, rid, topo.mask(core, to))
                sent[0] += len(topo.engines(core, to))
            x = task("G", emit, [], [c("SN%d" % t, lo, hi)], 200, (HOP if to in T.cores else HOPS) + (0 if t else FIRST))
            x["first"] = 3
            return x
        return [one(to, lo, hi) for to, (lo, hi) in zip(ways(t), parts_of(len(ways(t))))]

    def kappa():
        ts(c("K1", 0, 1), c("UP", 257, 258), 32.0, A.mult)
        ts(c("K2", 0, 1), c("K1", 0, 1), 1023, A.bitwise_and)
        cp(c("K3", 0, 1), c("K2", 0, 1))

    def moves():
        tt(w("DE"), w("HH"), c("EP", 0, 256), A.subtract)

    def flips(cl):
        e, sg = w("E%d" % cl), w("SG%d" % cl)
        ts(w("EB"), w("MI"), 16, A.arith_shift_right, 15, A.bitwise_and)
        tt(w("KV"), w("EB"), c("UP", 288, 304), A.max)
        tt(w("RX"), ind(w("KV"), w("CL")), w("RK"), A.mult)
        together([(c("VP", 0, 128), w("BH%d" % a1), c("RX", 128 * a1, 128 * a1 + 128), a1 == 0, a1 == 1) for a1 in (0, 1)])
        for par in (0, 1):
            ts(c("XP", 128 * par, 128 * par + 128), c("VP", 0, 128), later["won"][par], A.is_equal)
        tt(c("XP", 512, 768), c("XP", 0, 256), w("DE"), A.mult)
        hold.append(tasks[-1])
        act(c("ZP", 0, 256), c("XP", 0, 256), F.Copy, scale=-2.0, bias=1.0)
        hold.pop()
        tt(e, c("XP", 512, 768), e, A.add)
        tt(sg, c("ZP", 0, 256), sg, A.mult)

    def apply(t, own):
        src = T.cores[[r for r in range(n) if target(r, t, n) == rank][0]]
        hs = helpers(src, core, topo)
        ld = "LD%d" % t

        def lands(i, h, part):
            task("R", lambda: note("R", "arr%d_%d" % (i, t), len(topo.engines(h, core)), [], [part], {}), [part], [], 0, after=[own[i]])
        for i, (h, part) in enumerate(zip(hs or [src], parts_of(len(hs or [src])))):
            lands(i, h, c(ld, *part))
        of = c("UP", 272, 288)
        together([(of, w("I16"), c(ld, 0, 16), True, False), (of, w("IDN"), c(ld, 16, 32), False, True)], 2)
        ts(w("OU"), of, 4096.0, A.add)
        tt(w("SH"), ind(w("XH"), w("OU")), c(ld, 32, SW), A.add)
        scatter(w("TB"), w("OU"), w("SH"))

    first = len(tasks)
    first_lists(0, ((0, HEAD // 128),))
    negate(0, 1024)
    negate(1024, 2048)
    for x in tasks[first:]:
        x["first"] = 1
    first_lists(0, ((HEAD // 128, 4),))
    first = len(tasks)
    more_constants()
    for x in tasks[first:]:
        x["first"] = -1
    first_signs(0)
    shifted(c("EP", 0, 256), True)
    for x in tasks[-2:]:
        x["first"] = 3
    open_keys()
    for t in range(ROUNDS):
        cl, nx = t % 2, 1 - t % 2
        chains = {"e": hashes(cl, 0, 0, 2), "f": hashes(cl, 0, 2, 4), "g": hashes(cl, 1, 0, 2), "h": hashes(cl, 1, 2, 4)}
        steps = {"z": gather_z, "r": relu, "s": restart, "b": balances, "q": odd_amounts, "u": sum_u, "o": over, "c": count_over,
                 "w": sum_low, "y": far, "a": add_amounts, "k": minus, "m": plus, "j": sign_bank, "d": diff, "n": sign,
                 "p": score, "t": gate, "x": add_gate, "i": sign_half, "v": low_abs, "l": low_bits}
        fixed.extend("VSP")
        for step in ORDER.split():
            if step in chains:
                chains[step].pop(0)()
            else:
                steps[step[0]](*[int(x) if x.isdigit() else x for x in step[1:]])
            if step[0] == "z":
                tasks[-1]["first"] = 3
            if step == "q3" and t == 0:
                hold.append(tasks[-1])
                kept = fixed[:]
                del fixed[:]
                group_constants()
                for x in tasks[-4:]:
                    x["first"] = -1
                fixed.extend(kept)
                hold.pop()
        del fixed[:]
        hold.append([x for x in tasks if x["q"] == "S"][-1])
        for lo in range(0, EARLY, 256):
            halves(lo, lo + 256)
        hold.pop()
        if t == 0:
            iota(c("XH", 4096, TW), [[0, TW - 4096]], 0, 0)
        first = len(tasks)
        fixed.append("V")
        winners(t, parts_of(len(ways(t))))
        fixed.pop()
        for x in tasks[first:]:
            x["first"] = 3
        hold.extend(tasks[-2:])
        own = send(t)
        if t + 1 < ROUNDS:
            kappa()
        moves()
        if 0 < t < ROUNDS - 1:
            next_lists(nx)
            tasks[-1]["first"] = -1
        for lo in range(EARLY, 2048 if t else 4096, 256):
            halves(lo, lo + 256)
            tasks[-1]["first"] = -1
        if t == 0:
            spread_constants()
            first_lines(0)
            first_lists(1, ((0, 4),))
            first_signs(1)
            shifted(c("EP", 0, 256), False)
            first_lines(1)
        elif t + 1 < ROUNDS:
            shifted(w("E%d" % nx), False)
        first = len(tasks)
        apply(t, own)
        if t + 1 < ROUNDS:
            negate(0, 2048)
        for x in tasks[first:]:
            x["first"] = 3
        first = len(tasks)
        flips(cl)
        if t == 0:
            back_constants()
        if t + 2 >= ROUNDS:
            outputs(cl)
        for x in tasks[first + LATE:]:
            x["first"] = -1
        if t + 1 < ROUNDS:
            open_keys()
        del hold[:]
    dma("Y", "d5", T.yx[:], c("TB", 0, 2048), LOAD + 1200)
    dma("S", "d3", T.ym[:], w("YMB"), LOAD)
    dma("S", "d4", T.yl[:], w("YLB"), LOAD)
    issue()
    for d in ("d3", "d4", "d5"):
        g.sync.wait_ge(T.sem[d], 16)
    g.wait_ge(T.sem.loc, sent[0])
    for q in ("V", "S", "P", "G"):
        g.wait_ge(T.sem["q" + q], seq[q])
    for d in moved:
        if d not in ("d3", "d4", "d5"):
            g.wait_ge(T.sem[d], moved[d])
